import numpy as np
import ml_dtypes


def mxq(x, axis, fmt="e4m3"):
    dtype, down = {"e4m3": (ml_dtypes.float8_e4m3fn, 7), "e5m2": (ml_dtypes.float8_e5m2, 14)}[fmt]
    v = np.moveaxis(np.asarray(x, np.float32).astype(ml_dtypes.bfloat16).astype(np.float64), axis, -1)
    blocks = v.reshape(v.shape[:-1] + (-1, 32))
    amax = np.abs(blocks).max(-1, keepdims=True)
    byte = np.maximum(np.where(amax > 0, np.frexp(amax)[1] - 1 + 127, 0) - down, 1)
    scale = np.exp2(byte - 127.0)
    codes = (blocks / scale).astype(np.float32).astype(dtype).astype(np.float64)
    return np.moveaxis((codes * scale).reshape(v.shape), -1, axis)


WIDE = False


def mx_kscale(k):
    if not WIDE:
        return np.ones(k)
    levels = np.array([10, -10, 5, -5, 0])
    if k % 512:
        return np.exp2(np.random.permutation(np.resize(levels, k // 32))).repeat(32)
    a = np.empty((k // 512, 16))
    for p in range(k // 512):
        a[p, :8] = np.random.permutation(np.resize(levels, 8))
        for g in range(8):
            far = levels[np.abs(levels - a[p, g]) >= 10]
            a[p, g + 8] = far[np.random.randint(len(far))]
    return np.exp2(a.ravel()).repeat(32)


def f64(x):
    return np.asarray(x).astype(np.float64)


def striped(idx):
    return np.tile(idx.reshape(-1, 16).T, (8, 1)).astype(np.uint16)


def unstriped(offs):
    return offs[:16].T.reshape(-1).astype(np.int64)


E2M1 = np.array([0.0, 0.5, 1.0, 1.5, 2.0, 3.0, 4.0, 6.0, -0.0, -0.5, -1.0, -1.5, -2.0, -3.0, -4.0, -6.0])


def pack_fp4(w):
    k, n = w.shape
    w = f64(np.asarray(w, np.float32).astype(ml_dtypes.bfloat16)).reshape(k // 32, 32, n)
    amax = np.abs(w).max(1)
    mant, ex = np.frexp(amax / 6.0)
    byte = np.clip(np.where(amax > 0, np.where(mant > 0.5, ex, ex - 1) + 127, 1), 1, 254)
    scaled = (w * np.exp2(127.0 - byte)[:, None, :]).reshape(k, n).astype(np.float32)
    c = np.ascontiguousarray(scaled.reshape(k // 512, 128, 4, n).transpose(0, 1, 3, 2)).astype(ml_dtypes.float4_e2m1fn).view(np.uint8) & 0xF
    words = (c[..., 0::2] | (c[..., 1::2] << 4)).reshape(k // 512, 128, 2 * n)
    return np.ascontiguousarray(words), np.ascontiguousarray(byte.astype(np.uint8).reshape(k // 512, 16, n))


def unpack_fp4(words, scales):
    g, _, n = scales.shape
    words = np.ascontiguousarray(words).reshape(g, 128, n, 2)
    nib = np.empty((g, 128, n, 4), np.uint8)
    nib[..., 0::2] = words & 0xF
    nib[..., 1::2] = words >> 4
    vals = E2M1[nib] * np.repeat(np.exp2(scales.astype(np.float64) - 127.0), 8, axis=1)[..., None]
    return vals.transpose(0, 1, 3, 2).reshape(g * 512, n)


K, T, S, H, N = 1024, 1024, 512, 512, 128


def setup_inputs():
    n = np.random.standard_normal
    s = mx_kscale(K)[:, None]
    u = mx_kscale(H)
    packed_w1 = pack_fp4(n((K, N)) / np.sqrt(2 * K) / s)
    packed_w3 = pack_fp4(n((H, N)) / np.sqrt(2 * H) / u[:, None])
    return {
        "xT": (n((K, T)) * s).astype(np.float32),
        "w1_words": packed_w1[0],
        "w1_scales": packed_w1[1],
        "w2": (n((K, H)) / np.sqrt(K) / s * u).astype(np.float32),
        "w3_words": packed_w3[0],
        "w3_scales": packed_w3[1],
        "offs": striped(np.random.permutation(T)[:S]),
    }


def reference(xT, w1_words, w1_scales, w2, w3_words, w3_scales, offs):
    xq = mxq(f64(xT)[:, unstriped(offs)], 0, "e4m3")
    h = mxq(f64(w2), 0, "e4m3").T @ xq
    return unpack_fp4(w1_words, w1_scales).T @ xq + unpack_fp4(w3_words, w3_scales).T @ mxq(h, 0, "e4m3")

@@ -1,0 +1,181 @@
+from contextlib import ExitStack
+
+import concourse.mybir as mybir
+
+K, T, S, H, N = 1024, 1024, 512, 512, 128
+FLOPS = 2 * S * (K * H + K * N + H * N)
+
+F32 = mybir.dt.float32
+BF16 = mybir.dt.bfloat16
+I32 = mybir.dt.int32
+U32 = mybir.dt.uint32
+U16 = mybir.dt.uint16
+U8 = mybir.dt.uint8
+FP8X4 = mybir.dt.float8_e4m3fn_x4
+FP4X4 = mybir.dt.float4_e2m1fn_x4
+
+P = 128
+PACK = 4
+K_PASS = P * PACK
+PASSES = K // K_PASS
+GROUP = 128
+GROUPS = S // GROUP
+HALF_H = H // 2
+HALF_M = P // 2
+X_CHUNKS = [(0, 512), (512, 1024)]
+X_CHUNKS_LAST = [[0,512],[512,768],[768,1024]]
+SCALAR_COLS = {(0, 0): 256, (0, 1): 160, (1, 0): 168, (1, 1): 80}
+
+
+def tile_picked_lora_none_e_kernel(
+    tc, xT, w1_words, w1_scales, w2, w3_words, w3_scales, offs, out
+):
+    nc = tc.nc
+    with ExitStack() as ctx:
+        sb = ctx.enter_context(tc.tile_pool(name="sb", bufs=1))
+        psum = ctx.enter_context(tc.psum_pool(name="psum", bufs=1))
+
+        offsets = sb.tile([P, S // 16], U16, name="offsets")
+        w1_codes = sb.tile([P, PASSES, 2 * N], U8, name="w1_codes", align_bytes=64)
+        w3_codes = sb.tile([P, 2 * N], U8, name="w3_codes", align_bytes=64)
+        w1_sc = sb.tile([P, PASSES, N], U8, name="w1_sc", align_bytes=64)
+        w3_sc = sb.tile([P, N], U8, name="w3_sc", align_bytes=64)
+        nc.gpsimd.memset(w1_sc[:].bitcast(I32), 0)
+        nc.gpsimd.memset(w3_sc[:].bitcast(I32), 0)
+        small = [(w1_codes[:].bitcast(I32), w1_words.rearrange("z p c -> p z c").bitcast(I32))]
+        for q in range(4):
+            small.append((
+                w1_sc[32 * q : 32 * q + 4, :, :].bitcast(I32),
+                w1_scales[:, 4 * q : 4 * q + 4, :].rearrange("z r c -> r z c").bitcast(I32),
+            ))
+        small.append((w3_codes[:].bitcast(I32), w3_words[0].bitcast(I32)))
+        for q in range(4):
+            small.append((w3_sc[32 * q : 32 * q + 4, :].bitcast(I32), w3_scales[0, 4 * q : 4 * q + 4, :].bitcast(I32)))
+
+        def load_small(count, engine):
+            for dst, src in small[:count]:
+                engine.dma_start(out=dst, in_=src)
+            small[:count] = []
+
+
+        x_rows = xT.rearrange("(z p u e) t -> z u p e t", z=PASSES, p=P, u=2, e=2)
+        x_raw = {}
+        for z in range(PASSES):
+            for u in range(2):
+                chunks = X_CHUNKS_LAST if (z, u) == (PASSES - 1, 1) else X_CHUNKS
+                x_raw[z, u] = []
+                for lo, hi in chunks:
+                    raw = sb.tile([P, 2, hi - lo], F32, name="x_raw_%d_%d_%d" % (z, u, lo))
+                    nc.sync.dma_start(out=raw[:], in_=x_rows[z, u][:, :, lo:hi])
+                    x_raw[z, u].append((lo, hi, raw))
+                    if (z, u, lo) == (0, 0, 0):
+                        nc.sync.dma_start(offsets[:], offs)
+                    else:
+                        load_small(1, nc.sync)
+        w2_rows = w2.rearrange("(z p j) i -> z p j i", z=PASSES, p=P, j=PACK)
+        w2_raw = {}
+        for z in range(PASSES):
+            for c in range(2):
+                raw = sb.tile([P, PACK, HALF_H], F32, name="w2_raw_%d_%d" % (z, c))
+                nc.sync.dma_start(out=raw[:], in_=w2_rows[z][:, :, c * HALF_H : (c + 1) * HALF_H])
+                w2_raw[z, c] = raw
+                load_small(1, nc.sync)
+
+        x_codes, x_sc = [], []
+        for z in range(PASSES):
+            picked = sb.tile([P, S, 2], U32, name="picked_%d" % z, align_bytes=64)
+            for u in range(2):
+                pairs = sb.tile([P, T, 2], BF16, name="pairs_%d_%d" % (z, u), align_bytes=64)
+                for lo, hi, raw in x_raw[z, u]:
+                    nc.scalar.copy(out=pairs[:, lo:hi, :], in_=raw[:].rearrange("p e t -> p t e"))
+                window = pairs[:].rearrange("p t e -> p (t e)").bitcast(U32)
+                nc.vector.tensor_copy(out=picked[:, :, u], in_=window.indirect(offsets[:]))
+            codes = sb.tile([P, S], U32, name="x_codes_%d" % z, align_bytes=64)
+            sc = sb.tile([P, S], U8, name="x_sc_%d" % z, align_bytes=64)
+            nc.vector.quantize_mx(
+                out=codes[:].bitcast(FP8X4),
+                scales=sc[:],
+                in_=picked[:].rearrange("p s u -> p (s u)").bitcast(BF16),
+            )
+            x_codes.append(codes)
+            x_sc.append(sc)
+
+        out_acc = [psum.tile([P, GROUP], F32, name="out_acc_%d" % g) for g in range(GROUPS)]
+        for g in range(GROUPS):
+            cols = slice(g * GROUP, (g + 1) * GROUP)
+            for z in reversed(range(PASSES)):
+                nc.tensor.matmul_mx(
+                    out=out_acc[g][:],
+                    lhsT=w1_codes[:, z, :].bitcast(FP4X4),
+                    lhsT_scale=w1_sc[:, z, :],
+                    rhs=x_codes[z][:, cols].bitcast(FP8X4),
+                    rhs_scale=x_sc[z][:, cols],
+                    start=(z == PASSES - 1),
+                    stop=False,
+                )
+
+        def deal(engine_copy, grouped, raw, lo, hi):
+            if lo < hi:
+                engine_copy(
+                    out=grouped[:, :, lo // PACK : hi // PACK, :].rearrange("p t m j -> p m j t"),
+                    in_=raw[:, :, lo:hi].rearrange("p j (m t) -> p m j t", t=PACK),
+                )
+
+        h_acc = [psum.tile([P, PACK, GROUP], F32, name="h_acc_%d" % g) for g in range(GROUPS)]
+        for z in range(PASSES):
+            codes = sb.tile([P, PACK, P], U32, name="w2_codes_%d" % z, align_bytes=64)
+            sc = sb.tile([P, PACK, P], U8, name="w2_sc_%d" % z, align_bytes=64)
+            for c in range(2):
+                grouped = sb.tile([P, PACK, HALF_M, PACK], BF16, name="w2_grouped_%d_%d" % (z, c), align_bytes=64)
+                split = SCALAR_COLS[z, c]
+                deal(nc.scalar.copy, grouped, w2_raw[z, c], 0, split)
+                deal(nc.vector.tensor_copy, grouped, w2_raw[z, c], split, HALF_H)
+                for t in range(PACK):
+                    nc.vector.quantize_mx(
+                        out=codes[:, t, c * HALF_M : (c + 1) * HALF_M].bitcast(FP8X4),
+                        scales=sc[:, t, c * HALF_M : (c + 1) * HALF_M],
+                        in_=grouped[:, t, :, :].rearrange("p m j -> p (m j)"),
+                    )
+
+            if z == 0:
+                order = [(g, t) for t in range(PACK) for g in range(GROUPS)]
+            else:
+                order = [(g, t) for g in range(GROUPS) for t in range(PACK)]
+            for g, t in order:
+                cols = slice(g * GROUP, (g + 1) * GROUP)
+                nc.tensor.matmul_mx(
+                    out=h_acc[g][:, t, :],
+                    lhsT=codes[:, t, :].bitcast(FP8X4),
+                    lhsT_scale=sc[:, t, :],
+                    rhs=x_codes[z][:, cols].bitcast(FP8X4),
+                    rhs_scale=x_sc[z][:, cols],
+                    start=(z == 0 and t == 0),
+                    stop=(z == PASSES - 1 and t == PACK - 1),
+                )
+
+        h_bf = []
+        for g in range(GROUPS):
+            hb = sb.tile([P, GROUP, PACK], BF16, name="h_bf_%d" % g, align_bytes=64)
+            copy = nc.vector.tensor_copy if g in [1] else nc.scalar.copy
+            copy(out=hb[:], in_=h_acc[g][:].rearrange("p t n -> p n t"))
+            h_bf.append(hb)
+        for g in range(GROUPS):
+            cols = slice(g * GROUP, (g + 1) * GROUP)
+            codes = sb.tile([P, GROUP], U32, name="h_codes_%d" % g, align_bytes=64)
+            sc = sb.tile([P, GROUP], U8, name="h_sc_%d" % g, align_bytes=64)
+            nc.vector.quantize_mx(
+                out=codes[:].bitcast(FP8X4), scales=sc[:], in_=h_bf[g][:].rearrange("p n t -> p (n t)")
+            )
+            nc.tensor.matmul_mx(
+                out=out_acc[g][:],
+                lhsT=w3_codes[:].bitcast(FP4X4),
+                lhsT_scale=w3_sc[:],
+                rhs=codes[:].bitcast(FP8X4),
+                rhs_scale=sc[:],
+                start=False,
+                stop=True,
+            )
+            res = sb.tile([P, GROUP], F32, name="res_%d" % g)
+            copy = nc.vector.tensor_copy if g in [0,1] else nc.scalar.copy
+            copy(out=res[:], in_=out_acc[g][:])
+            nc.sync.dma_start(out=out[:, cols], in_=res[:])

@@ -24,7 +24,7 @@ HALF_H = H // 2
 HALF_M = P // 2
 X_CHUNKS = [(0, 512), (512, 1024)]
 X_CHUNKS_LAST = [[0,512],[512,768],[768,1024]]
-SCALAR_COLS = {(0, 0): 256, (0, 1): 160, (1, 0): 168, (1, 1): 80}
+LAST_SCALAR_COLS = 192
 
 
 def tile_picked_lora_none_e_kernel(
@@ -40,24 +40,13 @@ def tile_picked_lora_none_e_kernel(
         w3_codes = sb.tile([P, 2 * N], U8, name="w3_codes", align_bytes=64)
         w1_sc = sb.tile([P, PASSES, N], U8, name="w1_sc", align_bytes=64)
         w3_sc = sb.tile([P, N], U8, name="w3_sc", align_bytes=64)
-        nc.gpsimd.memset(w1_sc[:].bitcast(I32), 0)
-        nc.gpsimd.memset(w3_sc[:].bitcast(I32), 0)
-        small = [(w1_codes[:].bitcast(I32), w1_words.rearrange("z p c -> p z c").bitcast(I32))]
-        for q in range(4):
-            small.append((
-                w1_sc[32 * q : 32 * q + 4, :, :].bitcast(I32),
-                w1_scales[:, 4 * q : 4 * q + 4, :].rearrange("z r c -> r z c").bitcast(I32),
-            ))
-        small.append((w3_codes[:].bitcast(I32), w3_words[0].bitcast(I32)))
-        for q in range(4):
-            small.append((w3_sc[32 * q : 32 * q + 4, :].bitcast(I32), w3_scales[0, 4 * q : 4 * q + 4, :].bitcast(I32)))
+        nc.vector.memset(w1_sc[:].bitcast(I32), 0)
+        nc.vector.memset(w3_sc[:].bitcast(I32), 0)
 
-        def load_small(count, engine):
-            for dst, src in small[:count]:
-                engine.dma_start(out=dst, in_=src)
-            small[:count] = []
-
-
+        w2_rows = w2.rearrange("(z p j) i -> z p j i", z=PASSES, p=P, j=PACK)
+        w2_first = sb.tile([P, PACK, H], F32, name="w2_first")
+        nc.sync.dma_start(out=w2_first[:], in_=w2_rows[0])
+        nc.sync.dma_start(offsets[:], offs)
         x_rows = xT.rearrange("(z p u e) t -> z u p e t", z=PASSES, p=P, u=2, e=2)
         x_raw = {}
         for z in range(PASSES):
@@ -68,114 +57,148 @@ def tile_picked_lora_none_e_kernel(
                     raw = sb.tile([P, 2, hi - lo], F32, name="x_raw_%d_%d_%d" % (z, u, lo))
                     nc.sync.dma_start(out=raw[:], in_=x_rows[z, u][:, :, lo:hi])
                     x_raw[z, u].append((lo, hi, raw))
-                    if (z, u, lo) == (0, 0, 0):
-                        nc.sync.dma_start(offsets[:], offs)
-                    else:
-                        load_small(1, nc.sync)
-        w2_rows = w2.rearrange("(z p j) i -> z p j i", z=PASSES, p=P, j=PACK)
-        w2_raw = {}
-        for z in range(PASSES):
-            for c in range(2):
-                raw = sb.tile([P, PACK, HALF_H], F32, name="w2_raw_%d_%d" % (z, c))
-                nc.sync.dma_start(out=raw[:], in_=w2_rows[z][:, :, c * HALF_H : (c + 1) * HALF_H])
-                w2_raw[z, c] = raw
-                load_small(1, nc.sync)
-
-        x_codes, x_sc = [], []
-        for z in range(PASSES):
-            picked = sb.tile([P, S, 2], U32, name="picked_%d" % z, align_bytes=64)
-            for u in range(2):
-                pairs = sb.tile([P, T, 2], BF16, name="pairs_%d_%d" % (z, u), align_bytes=64)
-                for lo, hi, raw in x_raw[z, u]:
-                    nc.scalar.copy(out=pairs[:, lo:hi, :], in_=raw[:].rearrange("p e t -> p t e"))
-                window = pairs[:].rearrange("p t e -> p (t e)").bitcast(U32)
-                nc.vector.tensor_copy(out=picked[:, :, u], in_=window.indirect(offsets[:]))
-            codes = sb.tile([P, S], U32, name="x_codes_%d" % z, align_bytes=64)
-            sc = sb.tile([P, S], U8, name="x_sc_%d" % z, align_bytes=64)
-            nc.vector.quantize_mx(
-                out=codes[:].bitcast(FP8X4),
-                scales=sc[:],
-                in_=picked[:].rearrange("p s u -> p (s u)").bitcast(BF16),
+        w2_last = []
+        for c in range(2):
+            raw = sb.tile([P, PACK, HALF_H], F32, name="w2_last_%d" % c, tag="w2_last_%d" % c, align_bytes=64)
+            nc.sync.dma_start(out=raw[:], in_=w2_rows[1][:, :, c * HALF_H : (c + 1) * HALF_H])
+            w2_last.append(raw)
+        nc.sync.dma_start(out=w1_codes[:].bitcast(I32), in_=w1_words.rearrange("z p c -> p z c").bitcast(I32))
+        for q in range(4):
+            nc.sync.dma_start(
+                out=w1_sc[32 * q : 32 * q + 4, :, :].bitcast(I32),
+                in_=w1_scales[:, 4 * q : 4 * q + 4, :].rearrange("z r c -> r z c").bitcast(I32),
             )
-            x_codes.append(codes)
-            x_sc.append(sc)
+        nc.sync.dma_start(out=w3_codes[:].bitcast(I32), in_=w3_words[0].bitcast(I32))
+        for q in range(4):
+            nc.sync.dma_start(
+                out=w3_sc[32 * q : 32 * q + 4, :].bitcast(I32), in_=w3_scales[0, 4 * q : 4 * q + 4, :].bitcast(I32)
+            )
 
+        def deal(engine_copy, grouped, raw, lo, hi):
+            engine_copy(
+                out=grouped[:, :, lo // PACK : hi // PACK, :].rearrange("p t m j -> p m t j"),
+                in_=raw[:, :, lo:hi].rearrange("p j (m t) -> p m t j", t=PACK),
+            )
+
+        def quantize(codes, sc, values):
+            nc.vector.quantize_mx(out=codes.bitcast(FP8X4), scales=sc, in_=values)
+
+        grouped0 = sb.tile([P, PACK, P, PACK], BF16, name="w2_grouped_0", align_bytes=64)
+        deal(nc.scalar.copy, grouped0, w2_first, 0, 160)
+        deal(nc.vector.tensor_copy, grouped0, w2_first, 160, H)
+        w2_codes = {}
+        w2_sc = {}
+        for t in range(1, PACK):
+            w2_codes[0, t] = sb.tile([P, P], U32, name="w2_codes_0_%d" % t, align_bytes=64)
+            w2_sc[0, t] = sb.tile([P, P], U8, name="w2_sc_0_%d" % t, align_bytes=64)
+            quantize(w2_codes[0, t][:], w2_sc[0, t][:], grouped0[:, t, :, :].rearrange("p m j -> p (m j)"))
+
+        x_codes, x_sc, picked = {}, {}, []
+        for z in range(PASSES):
+            picked.append(sb.tile([P, S, 2], U32, name="picked_%d" % z, align_bytes=64))
+
+        def pick(z, u):
+            pairs = sb.tile([P, T, 2], BF16, name="pairs_%d_%d" % (z, u), tag="pairs_%d_%d" % (z, u), align_bytes=64)
+            for lo, hi, raw in x_raw[z, u]:
+                nc.scalar.copy(out=pairs[:, lo:hi, :], in_=raw[:].rearrange("p e t -> p t e"))
+            window = pairs[:].rearrange("p t e -> p (t e)").bitcast(U32)
+            nc.vector.tensor_copy(out=picked[z][:, :, u], in_=window.indirect(offsets[:]))
+
+        def quantize_x(z, g0, g1, tag):
+            codes = sb.tile([P, (g1 - g0) * GROUP], U32, name="x_codes_%d_%d" % (z, g0), tag=tag, align_bytes=64)
+            sc = sb.tile([P, (g1 - g0) * GROUP], U8, name="x_sc_%d_%d" % (z, g0), align_bytes=64)
+            words = picked[z][:, g0 * GROUP : g1 * GROUP, :].rearrange("p s u -> p (s u)")
+            quantize(codes[:], sc[:], words.bitcast(BF16))
+            for g in range(g0, g1):
+                cols = slice((g - g0) * GROUP, (g - g0 + 1) * GROUP)
+                x_codes[z, g] = codes[:, cols]
+                x_sc[z, g] = sc[:, cols]
+
+        h_acc = [psum.tile([P, PACK, GROUP], F32, name="h_acc_%d" % g) for g in range(GROUPS)]
         out_acc = [psum.tile([P, GROUP], F32, name="out_acc_%d" % g) for g in range(GROUPS)]
+
+        def h_pass(z, g, t):
+            nc.tensor.matmul_mx(
+                out=h_acc[g][:, t, :],
+                lhsT=w2_codes[z, t][:].bitcast(FP8X4),
+                lhsT_scale=w2_sc[z, t][:],
+                rhs=x_codes[z, g].bitcast(FP8X4),
+                rhs_scale=x_sc[z, g],
+                start=(z == 0 and t == 0),
+                stop=(z == PASSES - 1 and t == PACK - 1),
+            )
+
+        pick(0, 0)
+        pick(0, 1)
+        quantize_x(0, 0, GROUPS, "x_codes_0")
+        pick(1, 0)
+        w2_codes[0, 0] = sb.tile([P, P], U32, name="w2_codes_0_0", tag="pairs_1_0", align_bytes=64)
+        w2_sc[0, 0] = sb.tile([P, P], U8, name="w2_sc_0_0", align_bytes=64)
+        quantize(w2_codes[0, 0][:], w2_sc[0, 0][:], grouped0[:, 0, :, :].rearrange("p m j -> p (m j)"))
+        for t in range(PACK):
+            for g in range(GROUPS):
+                h_pass(0, g, t)
+        pick(1, 1)
+
+        for t in range(PACK):
+            w2_codes[1, t] = sb.tile([P, P], U32, name="w2_codes_1_%d" % t, align_bytes=64)
+            w2_sc[1, t] = sb.tile([P, P], U8, name="w2_sc_1_%d" % t, align_bytes=64)
+        for c in range(2):
+            grouped = sb.tile([P, PACK, HALF_M, PACK], BF16, name="w2_grouped_1_%d" % c, tag="w2_grouped_1_%d" % c, align_bytes=64)
+            if c == 0:
+                deal(nc.scalar.copy, grouped, w2_last[c], 0, HALF_H)
+            else:
+                deal(nc.scalar.copy, grouped, w2_last[c], 0, LAST_SCALAR_COLS)
+                deal(nc.vector.tensor_copy, grouped, w2_last[c], LAST_SCALAR_COLS, HALF_H)
+            half = slice(c * HALF_M, (c + 1) * HALF_M)
+            for t in range(PACK):
+                quantize(w2_codes[1, t][:, half], w2_sc[1, t][:, half], grouped[:, t, :, :].rearrange("p m j -> p (m j)"))
+            if c == 0:
+                quantize_x(1, 0, 1, "x_codes_1_0")
+        quantize_x(1, 1, 2, "w2_grouped_1_1")
+        quantize_x(1, 2, GROUPS, "w2_last_1")
+
         for g in range(GROUPS):
-            cols = slice(g * GROUP, (g + 1) * GROUP)
-            for z in reversed(range(PASSES)):
+            for t in range(PACK):
+                h_pass(1, g, t)
+
+        for g in range(GROUPS):
+            for z in range(PASSES):
                 nc.tensor.matmul_mx(
                     out=out_acc[g][:],
                     lhsT=w1_codes[:, z, :].bitcast(FP4X4),
                     lhsT_scale=w1_sc[:, z, :],
-                    rhs=x_codes[z][:, cols].bitcast(FP8X4),
-                    rhs_scale=x_sc[z][:, cols],
-                    start=(z == PASSES - 1),
+                    rhs=x_codes[z, g].bitcast(FP8X4),
+                    rhs_scale=x_sc[z, g],
+                    start=(z == 0),
                     stop=False,
                 )
 
-        def deal(engine_copy, grouped, raw, lo, hi):
-            if lo < hi:
-                engine_copy(
-                    out=grouped[:, :, lo // PACK : hi // PACK, :].rearrange("p t m j -> p m j t"),
-                    in_=raw[:, :, lo:hi].rearrange("p j (m t) -> p m j t", t=PACK),
-                )
+        h_bf = {}
+        spans = [(0, 2), (2, 3), (3, 4)]
+        for g0, g1 in spans:
+            hb = sb.tile([P, (g1 - g0) * GROUP, PACK], BF16, name="h_bf_%d" % g0, align_bytes=64)
+            h_bf[g0] = hb
+            for g in range(g0, g1):
+                copy = nc.vector.tensor_copy if g in [0,2] else nc.scalar.copy
+                copy(out=hb[:, (g - g0) * GROUP : (g - g0 + 1) * GROUP, :], in_=h_acc[g][:].rearrange("p t n -> p n t"))
 
-        h_acc = [psum.tile([P, PACK, GROUP], F32, name="h_acc_%d" % g) for g in range(GROUPS)]
-        for z in range(PASSES):
-            codes = sb.tile([P, PACK, P], U32, name="w2_codes_%d" % z, align_bytes=64)
-            sc = sb.tile([P, PACK, P], U8, name="w2_sc_%d" % z, align_bytes=64)
-            for c in range(2):
-                grouped = sb.tile([P, PACK, HALF_M, PACK], BF16, name="w2_grouped_%d_%d" % (z, c), align_bytes=64)
-                split = SCALAR_COLS[z, c]
-                deal(nc.scalar.copy, grouped, w2_raw[z, c], 0, split)
-                deal(nc.vector.tensor_copy, grouped, w2_raw[z, c], split, HALF_H)
-                for t in range(PACK):
-                    nc.vector.quantize_mx(
-                        out=codes[:, t, c * HALF_M : (c + 1) * HALF_M].bitcast(FP8X4),
-                        scales=sc[:, t, c * HALF_M : (c + 1) * HALF_M],
-                        in_=grouped[:, t, :, :].rearrange("p m j -> p (m j)"),
-                    )
-
-            if z == 0:
-                order = [(g, t) for t in range(PACK) for g in range(GROUPS)]
-            else:
-                order = [(g, t) for g in range(GROUPS) for t in range(PACK)]
-            for g, t in order:
-                cols = slice(g * GROUP, (g + 1) * GROUP)
+        for g0, g1 in spans:
+            codes = sb.tile([P, (g1 - g0) * GROUP], U32, name="h_codes_%d" % g0, align_bytes=64)
+            sc = sb.tile([P, (g1 - g0) * GROUP], U8, name="h_sc_%d" % g0, align_bytes=64)
+            quantize(codes[:], sc[:], h_bf[g0][:].rearrange("p n t -> p (n t)"))
+            for g in range(g0, g1):
+                cols = slice((g - g0) * GROUP, (g - g0 + 1) * GROUP)
                 nc.tensor.matmul_mx(
-                    out=h_acc[g][:, t, :],
-                    lhsT=codes[:, t, :].bitcast(FP8X4),
-                    lhsT_scale=sc[:, t, :],
-                    rhs=x_codes[z][:, cols].bitcast(FP8X4),
-                    rhs_scale=x_sc[z][:, cols],
-                    start=(z == 0 and t == 0),
-                    stop=(z == PASSES - 1 and t == PACK - 1),
+                    out=out_acc[g][:],
+                    lhsT=w3_codes[:].bitcast(FP4X4),
+                    lhsT_scale=w3_sc[:],
+                    rhs=codes[:, cols].bitcast(FP8X4),
+                    rhs_scale=sc[:, cols],
+                    start=False,
+                    stop=True,
                 )
-
-        h_bf = []
-        for g in range(GROUPS):
-            hb = sb.tile([P, GROUP, PACK], BF16, name="h_bf_%d" % g, align_bytes=64)
-            copy = nc.vector.tensor_copy if g in [1] else nc.scalar.copy
-            copy(out=hb[:], in_=h_acc[g][:].rearrange("p t n -> p n t"))
-            h_bf.append(hb)
-        for g in range(GROUPS):
-            cols = slice(g * GROUP, (g + 1) * GROUP)
-            codes = sb.tile([P, GROUP], U32, name="h_codes_%d" % g, align_bytes=64)
-            sc = sb.tile([P, GROUP], U8, name="h_sc_%d" % g, align_bytes=64)
-            nc.vector.quantize_mx(
-                out=codes[:].bitcast(FP8X4), scales=sc[:], in_=h_bf[g][:].rearrange("p n t -> p (n t)")
-            )
-            nc.tensor.matmul_mx(
-                out=out_acc[g][:],
-                lhsT=w3_codes[:].bitcast(FP4X4),
-                lhsT_scale=w3_sc[:],
-                rhs=codes[:].bitcast(FP8X4),
-                rhs_scale=sc[:],
-                start=False,
-                stop=True,
-            )
-            res = sb.tile([P, GROUP], F32, name="res_%d" % g)
-            copy = nc.vector.tensor_copy if g in [0,1] else nc.scalar.copy
-            copy(out=res[:], in_=out_acc[g][:])
-            nc.sync.dma_start(out=out[:, cols], in_=res[:])
+                res = sb.tile([P, GROUP], F32, name="res_%d" % g)
+                copy = nc.vector.tensor_copy if g in [3] else nc.scalar.copy
+                copy(out=res[:], in_=out_acc[g][:])
+                nc.sync.dma_start(out=out[:, g * GROUP : (g + 1) * GROUP], in_=res[:])

@@ -20,11 +20,12 @@ K_PASS = P * PACK
 PASSES = K // K_PASS
 GROUP = 128
 GROUPS = S // GROUP
+HALF_T = T // 2
+HALF_S = S // 2
 HALF_H = H // 2
 HALF_M = P // 2
-X_CHUNKS = [(0, 512), (512, 1024)]
-X_CHUNKS_LAST = [[0,512],[512,768],[768,1024]]
-LAST_SCALAR_COLS = 192
+X_SCALAR = {(0, 0): 176, (0, 1): 176, (1, 0): 352, (1, 1): 208}
+W2_PIECES = [[(0, 256, 256), (256, 512, 168)], [(0, 256, 136), (256, 384, 80), (384, 512, 48)]]
 
 
 def tile_picked_lora_none_e_kernel(
@@ -43,79 +44,108 @@ def tile_picked_lora_none_e_kernel(
         nc.vector.memset(w1_sc[:].bitcast(I32), 0)
         nc.vector.memset(w3_sc[:].bitcast(I32), 0)
 
-        w2_rows = w2.rearrange("(z p j) i -> z p j i", z=PASSES, p=P, j=PACK)
-        w2_first = sb.tile([P, PACK, H], F32, name="w2_first")
-        nc.sync.dma_start(out=w2_first[:], in_=w2_rows[0])
-        nc.sync.dma_start(offsets[:], offs)
         x_rows = xT.rearrange("(z p u e) t -> z u p e t", z=PASSES, p=P, u=2, e=2)
+        w2_rows = w2.rearrange("(z p j) i -> z p j i", z=PASSES, p=P, j=PACK)
         x_raw = {}
-        for z in range(PASSES):
-            for u in range(2):
-                chunks = X_CHUNKS_LAST if (z, u) == (PASSES - 1, 1) else X_CHUNKS
-                x_raw[z, u] = []
-                for lo, hi in chunks:
-                    raw = sb.tile([P, 2, hi - lo], F32, name="x_raw_%d_%d_%d" % (z, u, lo))
-                    nc.sync.dma_start(out=raw[:], in_=x_rows[z, u][:, :, lo:hi])
-                    x_raw[z, u].append((lo, hi, raw))
-        w2_last = []
-        for c in range(2):
-            raw = sb.tile([P, PACK, HALF_H], F32, name="w2_last_%d" % c, tag="w2_last_%d" % c, align_bytes=64)
-            nc.sync.dma_start(out=raw[:], in_=w2_rows[1][:, :, c * HALF_H : (c + 1) * HALF_H])
-            w2_last.append(raw)
-        nc.sync.dma_start(out=w1_codes[:].bitcast(I32), in_=w1_words.rearrange("z p c -> p z c").bitcast(I32))
+
+        def load_x(z, u, c):
+            x_raw[z, u, c] = sb.tile([P, 2, HALF_T], F32, name="x_raw_%d_%d_%d" % (z, u, c))
+            nc.sync.dma_start(out=x_raw[z, u, c][:], in_=x_rows[z, u][:, :, c * HALF_T : (c + 1) * HALF_T])
+
+        load_x(0, 0, 0)
+        load_x(0, 0, 1)
+        nc.sync.dma_start(offsets[:], offs)
+        load_x(0, 1, 0)
+        load_x(0, 1, 1)
         for q in range(4):
             nc.sync.dma_start(
                 out=w1_sc[32 * q : 32 * q + 4, :, :].bitcast(I32),
                 in_=w1_scales[:, 4 * q : 4 * q + 4, :].rearrange("z r c -> r z c").bitcast(I32),
             )
+        nc.sync.dma_start(out=w1_codes[:].bitcast(I32), in_=w1_words.rearrange("z p c -> p z c").bitcast(I32))
+        load_x(1, 0, 0)
+        load_x(1, 0, 1)
+        load_x(1, 1, 0)
+        load_x(1, 1, 1)
+        w2_raw = {}
+        for z in range(PASSES):
+            for lo, hi, cut in W2_PIECES[z]:
+                w2_raw[z, lo] = sb.tile([P, PACK, hi - lo], F32, name="w2_raw_%d_%d" % (z, lo))
+                nc.sync.dma_start(out=w2_raw[z, lo][:], in_=w2_rows[z][:, :, lo:hi])
         nc.sync.dma_start(out=w3_codes[:].bitcast(I32), in_=w3_words[0].bitcast(I32))
         for q in range(4):
             nc.sync.dma_start(
                 out=w3_sc[32 * q : 32 * q + 4, :].bitcast(I32), in_=w3_scales[0, 4 * q : 4 * q + 4, :].bitcast(I32)
             )
 
-        def deal(engine_copy, grouped, raw, lo, hi):
-            engine_copy(
-                out=grouped[:, :, lo // PACK : hi // PACK, :].rearrange("p t m j -> p m t j"),
-                in_=raw[:, :, lo:hi].rearrange("p j (m t) -> p m t j", t=PACK),
-            )
-
         def quantize(codes, sc, values):
             nc.vector.quantize_mx(out=codes.bitcast(FP8X4), scales=sc, in_=values)
-
-        grouped0 = sb.tile([P, PACK, P, PACK], BF16, name="w2_grouped_0", align_bytes=64)
-        deal(nc.scalar.copy, grouped0, w2_first, 0, 160)
-        deal(nc.vector.tensor_copy, grouped0, w2_first, 160, H)
-        w2_codes = {}
-        w2_sc = {}
-        for t in range(1, PACK):
-            w2_codes[0, t] = sb.tile([P, P], U32, name="w2_codes_0_%d" % t, align_bytes=64)
-            w2_sc[0, t] = sb.tile([P, P], U8, name="w2_sc_0_%d" % t, align_bytes=64)
-            quantize(w2_codes[0, t][:], w2_sc[0, t][:], grouped0[:, t, :, :].rearrange("p m j -> p (m j)"))
 
         x_codes, x_sc, picked = {}, {}, []
         for z in range(PASSES):
             picked.append(sb.tile([P, S, 2], U32, name="picked_%d" % z, align_bytes=64))
 
-        def pick(z, u):
-            pairs = sb.tile([P, T, 2], BF16, name="pairs_%d_%d" % (z, u), tag="pairs_%d_%d" % (z, u), align_bytes=64)
-            for lo, hi, raw in x_raw[z, u]:
-                nc.scalar.copy(out=pairs[:, lo:hi, :], in_=raw[:].rearrange("p e t -> p t e"))
+        def pick(z, u, slices):
+            pairs = sb.tile([P, T, 2], BF16, name="pairs_%d_%d" % (z, u), align_bytes=64)
+            cut = X_SCALAR[z, u]
+            for copy, c, lo, hi in (
+                (nc.scalar.copy, 0, 0, HALF_T),
+                (nc.scalar.copy, 1, 0, cut),
+                (nc.vector.tensor_copy, 1, cut, HALF_T),
+            ):
+                copy(
+                    out=pairs[:, c * HALF_T + lo : c * HALF_T + hi, :],
+                    in_=x_raw[z, u, c][:, :, lo:hi].rearrange("p e t -> p t e"),
+                )
             window = pairs[:].rearrange("p t e -> p (t e)").bitcast(U32)
-            nc.vector.tensor_copy(out=picked[z][:, :, u], in_=window.indirect(offsets[:]))
+            for lo, hi in slices:
+                nc.vector.tensor_copy(
+                    out=picked[z][:, lo:hi, u], in_=window.indirect(offsets[:, lo // 16 : hi // 16])
+                )
 
-        def quantize_x(z, g0, g1, tag):
-            codes = sb.tile([P, (g1 - g0) * GROUP], U32, name="x_codes_%d_%d" % (z, g0), tag=tag, align_bytes=64)
-            sc = sb.tile([P, (g1 - g0) * GROUP], U8, name="x_sc_%d_%d" % (z, g0), align_bytes=64)
-            words = picked[z][:, g0 * GROUP : g1 * GROUP, :].rearrange("p s u -> p (s u)")
+        def quantize_x(z, lo, hi):
+            codes = sb.tile([P, hi - lo], U32, name="x_codes_%d_%d" % (z, lo), align_bytes=64)
+            sc = sb.tile([P, hi - lo], U8, name="x_sc_%d_%d" % (z, lo), align_bytes=64)
+            words = picked[z][:, lo:hi, :].rearrange("p s u -> p (s u)")
             quantize(codes[:], sc[:], words.bitcast(BF16))
-            for g in range(g0, g1):
-                cols = slice((g - g0) * GROUP, (g - g0 + 1) * GROUP)
+            for g in range(lo // GROUP, hi // GROUP):
+                cols = slice(g * GROUP - lo, (g + 1) * GROUP - lo)
                 x_codes[z, g] = codes[:, cols]
                 x_sc[z, g] = sc[:, cols]
 
+        whole = [(0, S)]
+        halves = [(0, HALF_S), (HALF_S, S)]
+        pick(0, 0, whole)
+        pick(0, 1, whole)
+        quantize_x(0, 0, S)
+        pick(1, 0, whole)
+        pick(1, 1, halves)
+        for lo, hi in halves:
+            quantize_x(1, lo, hi)
+
         h_acc = [psum.tile([P, PACK, GROUP], F32, name="h_acc_%d" % g) for g in range(GROUPS)]
         out_acc = [psum.tile([P, GROUP], F32, name="out_acc_%d" % g) for g in range(GROUPS)]
+
+        for g in range(GROUPS):
+            for z in reversed(range(PASSES)):
+                nc.tensor.matmul_mx(
+                    out=out_acc[g][:],
+                    lhsT=w1_codes[:, z, :].bitcast(FP4X4),
+                    lhsT_scale=w1_sc[:, z, :],
+                    rhs=x_codes[z, g].bitcast(FP8X4),
+                    rhs_scale=x_sc[z, g],
+                    start=(z == PASSES - 1),
+                    stop=False,
+                )
+
+        w2_codes, w2_sc = {}, {}
+
+        def deal(copy, grouped, base, raw, piece_lo, lo, hi):
+            m0, m1 = (piece_lo + lo - base) // PACK, (piece_lo + hi - base) // PACK
+            copy(
+                out=grouped[:, :, m0:m1, :].rearrange("p t m j -> p m j t"),
+                in_=raw[:, :, lo:hi].rearrange("p j (m t) -> p m j t", t=PACK),
+            )
 
         def h_pass(z, g, t):
             nc.tensor.matmul_mx(
@@ -128,77 +158,53 @@ def tile_picked_lora_none_e_kernel(
                 stop=(z == PASSES - 1 and t == PACK - 1),
             )
 
-        pick(0, 0)
-        pick(0, 1)
-        quantize_x(0, 0, GROUPS, "x_codes_0")
-        pick(1, 0)
-        w2_codes[0, 0] = sb.tile([P, P], U32, name="w2_codes_0_0", tag="pairs_1_0", align_bytes=64)
-        w2_sc[0, 0] = sb.tile([P, P], U8, name="w2_sc_0_0", align_bytes=64)
-        quantize(w2_codes[0, 0][:], w2_sc[0, 0][:], grouped0[:, 0, :, :].rearrange("p m j -> p (m j)"))
-        for t in range(PACK):
-            for g in range(GROUPS):
-                h_pass(0, g, t)
-        pick(1, 1)
-
-        for t in range(PACK):
-            w2_codes[1, t] = sb.tile([P, P], U32, name="w2_codes_1_%d" % t, align_bytes=64)
-            w2_sc[1, t] = sb.tile([P, P], U8, name="w2_sc_1_%d" % t, align_bytes=64)
-        for c in range(2):
-            grouped = sb.tile([P, PACK, HALF_M, PACK], BF16, name="w2_grouped_1_%d" % c, tag="w2_grouped_1_%d" % c, align_bytes=64)
-            if c == 0:
-                deal(nc.scalar.copy, grouped, w2_last[c], 0, HALF_H)
+        for z in range(PASSES):
+            for t in range(PACK):
+                w2_codes[z, t] = sb.tile([P, P], U32, name="w2_codes_%d_%d" % (z, t), align_bytes=64)
+                w2_sc[z, t] = sb.tile([P, P], U8, name="w2_sc_%d_%d" % (z, t), align_bytes=64)
+            for c in range(2):
+                grouped = sb.tile([P, PACK, HALF_M, PACK], BF16, name="w2_grouped_%d_%d" % (z, c), align_bytes=64)
+                for lo, hi, cut in W2_PIECES[z]:
+                    if lo // HALF_H == c:
+                        if cut > 0:
+                            deal(nc.scalar.copy, grouped, c * HALF_H, w2_raw[z, lo], lo, 0, cut)
+                        if cut < hi - lo:
+                            deal(nc.vector.tensor_copy, grouped, c * HALF_H, w2_raw[z, lo], lo, cut, hi - lo)
+                half = slice(c * HALF_M, (c + 1) * HALF_M)
+                for t in range(PACK):
+                    quantize(
+                        w2_codes[z, t][:, half], w2_sc[z, t][:, half], grouped[:, t, :, :].rearrange("p m j -> p (m j)")
+                    )
+            if z == 0:
+                for t in range(PACK):
+                    for g in range(GROUPS):
+                        h_pass(z, g, t)
             else:
-                deal(nc.scalar.copy, grouped, w2_last[c], 0, LAST_SCALAR_COLS)
-                deal(nc.vector.tensor_copy, grouped, w2_last[c], LAST_SCALAR_COLS, HALF_H)
-            half = slice(c * HALF_M, (c + 1) * HALF_M)
-            for t in range(PACK):
-                quantize(w2_codes[1, t][:, half], w2_sc[1, t][:, half], grouped[:, t, :, :].rearrange("p m j -> p (m j)"))
-            if c == 0:
-                quantize_x(1, 0, 1, "x_codes_1_0")
-        quantize_x(1, 1, 2, "w2_grouped_1_1")
-        quantize_x(1, 2, GROUPS, "w2_last_1")
+                for g in range(GROUPS):
+                    for t in range(PACK):
+                        h_pass(z, g, t)
+
+        h_bf = []
+        for g in range(GROUPS):
+            hb = sb.tile([P, GROUP, PACK], BF16, name="h_bf_%d" % g, align_bytes=64)
+            h_bf.append(hb)
+            copy = nc.vector.tensor_copy if g % 2 == 0 else nc.scalar.copy
+            copy(out=hb[:], in_=h_acc[g][:].rearrange("p t n -> p n t"))
 
         for g in range(GROUPS):
-            for t in range(PACK):
-                h_pass(1, g, t)
-
-        for g in range(GROUPS):
-            for z in range(PASSES):
-                nc.tensor.matmul_mx(
-                    out=out_acc[g][:],
-                    lhsT=w1_codes[:, z, :].bitcast(FP4X4),
-                    lhsT_scale=w1_sc[:, z, :],
-                    rhs=x_codes[z, g].bitcast(FP8X4),
-                    rhs_scale=x_sc[z, g],
-                    start=(z == 0),
-                    stop=False,
-                )
-
-        h_bf = {}
-        spans = [(0, 2), (2, 3), (3, 4)]
-        for g0, g1 in spans:
-            hb = sb.tile([P, (g1 - g0) * GROUP, PACK], BF16, name="h_bf_%d" % g0, align_bytes=64)
-            h_bf[g0] = hb
-            for g in range(g0, g1):
-                copy = nc.vector.tensor_copy if g in [0,2] else nc.scalar.copy
-                copy(out=hb[:, (g - g0) * GROUP : (g - g0 + 1) * GROUP, :], in_=h_acc[g][:].rearrange("p t n -> p n t"))
-
-        for g0, g1 in spans:
-            codes = sb.tile([P, (g1 - g0) * GROUP], U32, name="h_codes_%d" % g0, align_bytes=64)
-            sc = sb.tile([P, (g1 - g0) * GROUP], U8, name="h_sc_%d" % g0, align_bytes=64)
-            quantize(codes[:], sc[:], h_bf[g0][:].rearrange("p n t -> p (n t)"))
-            for g in range(g0, g1):
-                cols = slice((g - g0) * GROUP, (g - g0 + 1) * GROUP)
-                nc.tensor.matmul_mx(
-                    out=out_acc[g][:],
-                    lhsT=w3_codes[:].bitcast(FP4X4),
-                    lhsT_scale=w3_sc[:],
-                    rhs=codes[:, cols].bitcast(FP8X4),
-                    rhs_scale=sc[:, cols],
-                    start=False,
-                    stop=True,
-                )
-                res = sb.tile([P, GROUP], F32, name="res_%d" % g)
-                copy = nc.vector.tensor_copy if g in [3] else nc.scalar.copy
-                copy(out=res[:], in_=out_acc[g][:])
-                nc.sync.dma_start(out=out[:, g * GROUP : (g + 1) * GROUP], in_=res[:])
+            codes = sb.tile([P, GROUP], U32, name="h_codes_%d" % g, align_bytes=64)
+            sc = sb.tile([P, GROUP], U8, name="h_sc_%d" % g, align_bytes=64)
+            quantize(codes[:], sc[:], h_bf[g][:].rearrange("p n t -> p (n t)"))
+            nc.tensor.matmul_mx(
+                out=out_acc[g][:],
+                lhsT=w3_codes[:].bitcast(FP4X4),
+                lhsT_scale=w3_sc[:],
+                rhs=codes[:].bitcast(FP8X4),
+                rhs_scale=sc[:],
+                start=False,
+                stop=True,
+            )
+            res = sb.tile([P, GROUP], F32, name="res_%d" % g)
+            copy = nc.vector.tensor_copy if g == GROUPS - 1 else nc.scalar.copy
+            copy(out=res[:], in_=out_acc[g][:])
+            nc.sync.dma_start(out=out[:, g * GROUP : (g + 1) * GROUP], in_=res[:])

@@ -37,8 +37,8 @@ def tile_picked_lora_none_e_kernel(
         psum = ctx.enter_context(tc.psum_pool(name="psum", bufs=1))
 
         offsets = sb.tile([P, S // 16], U16, name="offsets")
-        w1_codes = sb.tile([P, PASSES, 2 * N], U8, name="w1_codes", align_bytes=64)
-        w3_codes = sb.tile([P, 2 * N], U8, name="w3_codes", align_bytes=64)
+        w1_codes = sb.tile([P, PASSES, 2 * N], U8, name="w1_codes", align_bytes=256)
+        w3_codes = sb.tile([P, 2 * N], U8, name="w3_codes", align_bytes=256)
         w1_sc = sb.tile([P, PASSES, N], U8, name="w1_sc", align_bytes=64)
         w3_sc = sb.tile([P, N], U8, name="w3_sc", align_bytes=64)
         nc.vector.memset(w1_sc[:].bitcast(I32), 0)
@@ -49,7 +49,7 @@ def tile_picked_lora_none_e_kernel(
         x_raw = {}
 
         def load_x(z, u, c):
-            x_raw[z, u, c] = sb.tile([P, 2, HALF_T], F32, name="x_raw_%d_%d_%d" % (z, u, c))
+            x_raw[z, u, c] = sb.tile([P, 2, HALF_T], F32, name="x_raw_%d_%d_%d" % (z, u, c), align_bytes=256)
             nc.sync.dma_start(out=x_raw[z, u, c][:], in_=x_rows[z, u][:, :, c * HALF_T : (c + 1) * HALF_T])
 
         load_x(0, 0, 0)
@@ -70,7 +70,7 @@ def tile_picked_lora_none_e_kernel(
         w2_raw = {}
         for z in range(PASSES):
             for lo, hi, cut in W2_PIECES[z]:
-                w2_raw[z, lo] = sb.tile([P, PACK, hi - lo], F32, name="w2_raw_%d_%d" % (z, lo))
+                w2_raw[z, lo] = sb.tile([P, PACK, hi - lo], F32, name="w2_raw_%d_%d" % (z, lo), align_bytes=256)
                 nc.sync.dma_start(out=w2_raw[z, lo][:], in_=w2_rows[z][:, :, lo:hi])
         nc.sync.dma_start(out=w3_codes[:].bitcast(I32), in_=w3_words[0].bitcast(I32))
         for q in range(4):
@@ -204,7 +204,7 @@ def tile_picked_lora_none_e_kernel(
                 start=False,
                 stop=True,
             )
-            res = sb.tile([P, GROUP], F32, name="res_%d" % g)
+            res = sb.tile([P, GROUP], F32, name="res_%d" % g, align_bytes=256)
             copy = nc.vector.tensor_copy if g == GROUPS - 1 else nc.scalar.copy
             copy(out=res[:], in_=out_acc[g][:])
             nc.sync.dma_start(out=out[:, g * GROUP : (g + 1) * GROUP], in_=res[:])

@@ -20,12 +20,18 @@ K_PASS = P * PACK
 PASSES = K // K_PASS
 GROUP = 128
 GROUPS = S // GROUP
-HALF_T = T // 2
 HALF_S = S // 2
 HALF_H = H // 2
-HALF_M = P // 2
-X_SCALAR = {(0, 0): 176, (0, 1): 176, (1, 0): 352, (1, 1): 208}
-W2_PIECES = [[(0, 256, 256), (256, 512, 168)], [(0, 256, 136), (256, 384, 80), (384, 512, 48)]]
+X_PIECES = {
+    (0, 0): [(0, 512, 512), (512, 1024, 688)],
+    (0, 1): [(0, 512, 512), (512, 1024, 688)],
+    (1, 0): [(0, 512, 512), (512, 1024, 832)],
+    (1, 1): [(0, 512, 512), (512, 1024, 688)],
+}
+W2_PIECES = [
+    [(0, 256, 256), (256, 512, 408)],
+    [(0, 256, 136), (256, 384, 320), (384, 512, 432)],
+]
 
 
 def tile_picked_lora_none_e_kernel(
@@ -46,32 +52,33 @@ def tile_picked_lora_none_e_kernel(
 
         x_rows = xT.rearrange("(z p u e) t -> z u p e t", z=PASSES, p=P, u=2, e=2)
         w2_rows = w2.rearrange("(z p j) i -> z p j i", z=PASSES, p=P, j=PACK)
-        x_raw = {}
+        x_raw, w2_raw = {}, {}
 
-        def load_x(z, u, c):
-            x_raw[z, u, c] = sb.tile([P, 2, HALF_T], F32, name="x_raw_%d_%d_%d" % (z, u, c), align_bytes=256)
-            nc.sync.dma_start(out=x_raw[z, u, c][:], in_=x_rows[z, u][:, :, c * HALF_T : (c + 1) * HALF_T])
+        def load_x(z, u):
+            for lo, hi, cut in X_PIECES[z, u]:
+                x_raw[z, u, lo] = sb.tile([P, 2, hi - lo], F32, name="x_raw_%d_%d_%d" % (z, u, lo), align_bytes=256)
+                nc.sync.dma_start(out=x_raw[z, u, lo][:], in_=x_rows[z, u][:, :, lo:hi])
 
-        load_x(0, 0, 0)
-        load_x(0, 0, 1)
+        def load_w2(z, pieces):
+            for lo, hi, cut in pieces:
+                name = "w2_raw_%d_%d" % (z, lo)
+                w2_raw[z, lo] = sb.tile([P, PACK, hi - lo], F32, name=name, tag=name, align_bytes=256)
+                nc.sync.dma_start(out=w2_raw[z, lo][:], in_=w2_rows[z][:, :, lo:hi])
+
+        load_x(0, 0)
         nc.sync.dma_start(offsets[:], offs)
-        load_x(0, 1, 0)
-        load_x(0, 1, 1)
+        load_x(0, 1)
         for q in range(4):
             nc.sync.dma_start(
                 out=w1_sc[32 * q : 32 * q + 4, :, :].bitcast(I32),
                 in_=w1_scales[:, 4 * q : 4 * q + 4, :].rearrange("z r c -> r z c").bitcast(I32),
             )
         nc.sync.dma_start(out=w1_codes[:].bitcast(I32), in_=w1_words.rearrange("z p c -> p z c").bitcast(I32))
-        load_x(1, 0, 0)
-        load_x(1, 0, 1)
-        load_x(1, 1, 0)
-        load_x(1, 1, 1)
-        w2_raw = {}
-        for z in range(PASSES):
-            for lo, hi, cut in W2_PIECES[z]:
-                w2_raw[z, lo] = sb.tile([P, PACK, hi - lo], F32, name="w2_raw_%d_%d" % (z, lo), align_bytes=256)
-                nc.sync.dma_start(out=w2_raw[z, lo][:], in_=w2_rows[z][:, :, lo:hi])
+        load_x(1, 0)
+        load_w2(0, W2_PIECES[0][:0])
+        load_x(1, 1)
+        load_w2(0, W2_PIECES[0][0:])
+        load_w2(1, W2_PIECES[1])
         nc.sync.dma_start(out=w3_codes[:].bitcast(I32), in_=w3_words[0].bitcast(I32))
         for q in range(4):
             nc.sync.dma_start(
@@ -81,108 +88,113 @@ def tile_picked_lora_none_e_kernel(
         def quantize(codes, sc, values):
             nc.vector.quantize_mx(out=codes.bitcast(FP8X4), scales=sc, in_=values)
 
-        x_codes, x_sc, picked = {}, {}, []
-        for z in range(PASSES):
-            picked.append(sb.tile([P, S, 2], U32, name="picked_%d" % z, align_bytes=64))
-
-        def pick(z, u, slices):
+        def round_pairs(z, u):
             pairs = sb.tile([P, T, 2], BF16, name="pairs_%d_%d" % (z, u), align_bytes=64)
-            cut = X_SCALAR[z, u]
-            for copy, c, lo, hi in (
-                (nc.scalar.copy, 0, 0, HALF_T),
-                (nc.scalar.copy, 1, 0, cut),
-                (nc.vector.tensor_copy, 1, cut, HALF_T),
-            ):
-                copy(
-                    out=pairs[:, c * HALF_T + lo : c * HALF_T + hi, :],
-                    in_=x_raw[z, u, c][:, :, lo:hi].rearrange("p e t -> p t e"),
-                )
-            window = pairs[:].rearrange("p t e -> p (t e)").bitcast(U32)
-            for lo, hi in slices:
-                nc.vector.tensor_copy(
-                    out=picked[z][:, lo:hi, u], in_=window.indirect(offsets[:, lo // 16 : hi // 16])
-                )
+            for lo, hi, cut in X_PIECES[z, u]:
+                for copy, a, b in ((nc.scalar.copy, lo, cut), (nc.vector.tensor_copy, cut, hi)):
+                    if a < b:
+                        copy(out=pairs[:, a:b, :], in_=x_raw[z, u, lo][:, :, a - lo : b - lo].rearrange("p e t -> p t e"))
+            return pairs[:].rearrange("p t e -> p (t e)").bitcast(U32)
 
-        def quantize_x(z, lo, hi):
-            codes = sb.tile([P, hi - lo], U32, name="x_codes_%d_%d" % (z, lo), align_bytes=64)
+        def gather(dst, window, lo, hi):
+            nc.vector.tensor_copy(out=dst, in_=window.indirect(offsets[:, lo // 16 : hi // 16]))
+
+        x_codes, x_sc = {}, {}
+
+        def quantize_x(z, lo, hi, words, tag):
+            codes = sb.tile([P, hi - lo], U32, name="x_codes_%d_%d" % (z, lo), tag=tag, align_bytes=256)
             sc = sb.tile([P, hi - lo], U8, name="x_sc_%d_%d" % (z, lo), align_bytes=64)
-            words = picked[z][:, lo:hi, :].rearrange("p s u -> p (s u)")
-            quantize(codes[:], sc[:], words.bitcast(BF16))
+            quantize(codes[:], sc[:], words.rearrange("p s u -> p (s u)").bitcast(BF16))
             for g in range(lo // GROUP, hi // GROUP):
                 cols = slice(g * GROUP - lo, (g + 1) * GROUP - lo)
                 x_codes[z, g] = codes[:, cols]
                 x_sc[z, g] = sc[:, cols]
 
-        whole = [(0, S)]
-        halves = [(0, HALF_S), (HALF_S, S)]
-        pick(0, 0, whole)
-        pick(0, 1, whole)
-        quantize_x(0, 0, S)
-        pick(1, 0, whole)
-        pick(1, 1, halves)
-        for lo, hi in halves:
-            quantize_x(1, lo, hi)
+        w2_codes, w2_sc = {}, {}
+
+        def prepare_w2(z, spans):
+            codes = sb.tile([P, PACK, P], U32, name="w2_codes_%d" % z, align_bytes=64)
+            sc = sb.tile([P, PACK, P], U8, name="w2_sc_%d" % z, align_bytes=64)
+            for t in range(PACK):
+                w2_codes[z, t] = codes[:, t, :]
+                w2_sc[z, t] = sc[:, t, :]
+            for c0, c1 in spans:
+                name = "w2_grouped_%d_%d" % (z, c0)
+                grouped = sb.tile([P, PACK, (c1 - c0) // PACK, PACK], BF16, name=name, tag=name, align_bytes=64)
+                for lo, hi, cut in W2_PIECES[z]:
+                    for copy, a, b in ((nc.scalar.copy, lo, cut), (nc.vector.tensor_copy, cut, hi)):
+                        if c0 <= a < b <= c1:
+                            copy(
+                                out=grouped[:, :, (a - c0) // PACK : (b - c0) // PACK, :].rearrange("p t m j -> p m j t"),
+                                in_=w2_raw[z, lo][:, :, a - lo : b - lo].rearrange("p j (m t) -> p m j t", t=PACK),
+                            )
+                if c1 - c0 == H:
+                    quantize(
+                        codes[:].rearrange("p t m -> p (t m)"),
+                        sc[:].rearrange("p t m -> p (t m)"),
+                        grouped[:].rearrange("p t m j -> p (t m j)"),
+                    )
+                else:
+                    cols = slice(c0 // PACK, c1 // PACK)
+                    for t in range(PACK):
+                        quantize(codes[:, t, cols], sc[:, t, cols], grouped[:, t, :, :].rearrange("p m j -> p (m j)"))
 
         h_acc = [psum.tile([P, PACK, GROUP], F32, name="h_acc_%d" % g) for g in range(GROUPS)]
         out_acc = [psum.tile([P, GROUP], F32, name="out_acc_%d" % g) for g in range(GROUPS)]
 
-        for g in range(GROUPS):
-            for z in reversed(range(PASSES)):
-                nc.tensor.matmul_mx(
-                    out=out_acc[g][:],
-                    lhsT=w1_codes[:, z, :].bitcast(FP4X4),
-                    lhsT_scale=w1_sc[:, z, :],
-                    rhs=x_codes[z, g].bitcast(FP8X4),
-                    rhs_scale=x_sc[z, g],
-                    start=(z == PASSES - 1),
-                    stop=False,
-                )
-
-        w2_codes, w2_sc = {}, {}
-
-        def deal(copy, grouped, base, raw, piece_lo, lo, hi):
-            m0, m1 = (piece_lo + lo - base) // PACK, (piece_lo + hi - base) // PACK
-            copy(
-                out=grouped[:, :, m0:m1, :].rearrange("p t m j -> p m j t"),
-                in_=raw[:, :, lo:hi].rearrange("p j (m t) -> p m j t", t=PACK),
-            )
-
         def h_pass(z, g, t):
             nc.tensor.matmul_mx(
                 out=h_acc[g][:, t, :],
-                lhsT=w2_codes[z, t][:].bitcast(FP8X4),
-                lhsT_scale=w2_sc[z, t][:],
+                lhsT=w2_codes[z, t].bitcast(FP8X4),
+                lhsT_scale=w2_sc[z, t],
                 rhs=x_codes[z, g].bitcast(FP8X4),
                 rhs_scale=x_sc[z, g],
                 start=(z == 0 and t == 0),
                 stop=(z == PASSES - 1 and t == PACK - 1),
             )
 
+        def w1_pass(z, g):
+            nc.tensor.matmul_mx(
+                out=out_acc[g][:],
+                lhsT=w1_codes[:, z, :].bitcast(FP4X4),
+                lhsT_scale=w1_sc[:, z, :],
+                rhs=x_codes[z, g].bitcast(FP8X4),
+                rhs_scale=x_sc[z, g],
+                start=(z == PASSES - 1),
+                stop=False,
+            )
+
+        halves = [(0, HALF_S), (HALF_S, S)]
         for z in range(PASSES):
+            gathered = sb.tile([P, 2, S], U32, name="gathered_%d" % z, align_bytes=64)
+            picked = sb.tile([P, S, 2], U32, name="picked_%d" % z, align_bytes=64)
+            gather(gathered[:, 0, :], round_pairs(z, 0), 0, S)
+            window = round_pairs(z, 1)
+            for lo, hi in halves:
+                gather(gathered[:, 1, lo:hi], window, lo, hi)
+            for lo, hi in halves:
+                nc.vector.tensor_copy(
+                    out=picked[:, lo:hi, :].bitcast(I32),
+                    in_=gathered[:, :, lo:hi].bitcast(I32).rearrange("p u s -> p s u"),
+                )
+            for lo, hi in halves if z == 0 else halves[:1]:
+                quantize_x(z, lo, hi, picked[:, lo:hi, :], "x_codes_%d_%d" % (z, lo))
+
+        for g in range(2):
+            for z in reversed(range(PASSES)):
+                w1_pass(z, g)
+        prepare_w2(0, [(0, HALF_H), (HALF_H, H)])
+        for t in range(PACK):
+            for g in range(GROUPS):
+                h_pass(0, g, t)
+        prepare_w2(1, [(0, HALF_H), (HALF_H, H)])
+        quantize_x(1, HALF_S, S, picked[:, HALF_S:, :], "w2_raw_1_%d" % W2_PIECES[1][-1][0])
+        for g in range(GROUPS):
             for t in range(PACK):
-                w2_codes[z, t] = sb.tile([P, P], U32, name="w2_codes_%d_%d" % (z, t), align_bytes=64)
-                w2_sc[z, t] = sb.tile([P, P], U8, name="w2_sc_%d_%d" % (z, t), align_bytes=64)
-            for c in range(2):
-                grouped = sb.tile([P, PACK, HALF_M, PACK], BF16, name="w2_grouped_%d_%d" % (z, c), align_bytes=64)
-                for lo, hi, cut in W2_PIECES[z]:
-                    if lo // HALF_H == c:
-                        if cut > 0:
-                            deal(nc.scalar.copy, grouped, c * HALF_H, w2_raw[z, lo], lo, 0, cut)
-                        if cut < hi - lo:
-                            deal(nc.vector.tensor_copy, grouped, c * HALF_H, w2_raw[z, lo], lo, cut, hi - lo)
-                half = slice(c * HALF_M, (c + 1) * HALF_M)
-                for t in range(PACK):
-                    quantize(
-                        w2_codes[z, t][:, half], w2_sc[z, t][:, half], grouped[:, t, :, :].rearrange("p m j -> p (m j)")
-                    )
-            if z == 0:
-                for t in range(PACK):
-                    for g in range(GROUPS):
-                        h_pass(z, g, t)
-            else:
-                for g in range(GROUPS):
-                    for t in range(PACK):
-                        h_pass(z, g, t)
+                h_pass(1, g, t)
+        for g in range(2, GROUPS):
+            for z in reversed(range(PASSES)):
+                w1_pass(z, g)
 
         h_bf = []
         for g in range(GROUPS):

@@ -25,12 +25,12 @@ HALF_H = H // 2
 X_PIECES = {
     (0, 0): [(0, 512, 512), (512, 1024, 688)],
     (0, 1): [(0, 512, 512), (512, 1024, 688)],
-    (1, 0): [(0, 512, 512), (512, 1024, 832)],
-    (1, 1): [(0, 512, 512), (512, 1024, 688)],
+    (1, 0): [(0, 512, 512), (512, 1024, 896)],
+    (1, 1): [(0, 512, 512), (512, 1024, 720)],
 }
 W2_PIECES = [
-    [(0, 256, 256), (256, 512, 408)],
-    [(0, 256, 136), (256, 384, 320), (384, 512, 432)],
+    [(0, 256, 256), (256, 512, 432)],
+    [(0, 256, 160), (256, 384, 320), (384, 512, 432)],
 ]
 
 
@@ -73,11 +73,11 @@ def tile_picked_lora_none_e_kernel(
                 out=w1_sc[32 * q : 32 * q + 4, :, :].bitcast(I32),
                 in_=w1_scales[:, 4 * q : 4 * q + 4, :].rearrange("z r c -> r z c").bitcast(I32),
             )
-        nc.sync.dma_start(out=w1_codes[:].bitcast(I32), in_=w1_words.rearrange("z p c -> p z c").bitcast(I32))
         load_x(1, 0)
         load_w2(0, W2_PIECES[0][:0])
         load_x(1, 1)
         load_w2(0, W2_PIECES[0][0:])
+        nc.sync.dma_start(out=w1_codes[:].bitcast(I32), in_=w1_words.rearrange("z p c -> p z c").bitcast(I32))
         load_w2(1, W2_PIECES[1])
         nc.sync.dma_start(out=w3_codes[:].bitcast(I32), in_=w3_words[0].bitcast(I32))
         for q in range(4):
@@ -100,11 +100,16 @@ def tile_picked_lora_none_e_kernel(
             nc.vector.tensor_copy(out=dst, in_=window.indirect(offsets[:, lo // 16 : hi // 16]))
 
         x_codes, x_sc = {}, {}
+        first_codes = sb.tile([P, S], U32, name="first_codes", align_bytes=256)
+        first_sc = sb.tile([P, S], U8, name="first_sc", align_bytes=64)
 
         def quantize_x(z, lo, hi, words, tag):
-            codes = sb.tile([P, hi - lo], U32, name="x_codes_%d_%d" % (z, lo), tag=tag, align_bytes=256)
-            sc = sb.tile([P, hi - lo], U8, name="x_sc_%d_%d" % (z, lo), align_bytes=64)
-            quantize(codes[:], sc[:], words.rearrange("p s u -> p (s u)").bitcast(BF16))
+            if z == 0:
+                codes, sc = first_codes[:, lo:hi], first_sc[:, lo:hi]
+            else:
+                codes = sb.tile([P, hi - lo], U32, name="x_codes_%d_%d" % (z, lo), tag=tag, align_bytes=256)[:]
+                sc = sb.tile([P, hi - lo], U8, name="x_sc_%d_%d" % (z, lo), align_bytes=64)[:]
+            quantize(codes, sc, words.rearrange("p s u -> p (s u)").bitcast(BF16))
             for g in range(lo // GROUP, hi // GROUP):
                 cols = slice(g * GROUP - lo, (g + 1) * GROUP - lo)
                 x_codes[z, g] = codes[:, cols]
@@ -160,7 +165,7 @@ def tile_picked_lora_none_e_kernel(
                 lhsT_scale=w1_sc[:, z, :],
                 rhs=x_codes[z, g].bitcast(FP8X4),
                 rhs_scale=x_sc[z, g],
-                start=(z == PASSES - 1),
+                start=(z == 0),
                 stop=False,
             )
 
@@ -181,8 +186,19 @@ def tile_picked_lora_none_e_kernel(
                 quantize_x(z, lo, hi, picked[:, lo:hi, :], "x_codes_%d_%d" % (z, lo))
 
         for g in range(2):
-            for z in reversed(range(PASSES)):
-                w1_pass(z, g)
+            nc.tensor.matmul_mx(
+                out=h_acc[g][:].rearrange("p t n -> p (t n)"),
+                lhsT=w1_codes[:, 0, :].bitcast(FP4X4),
+                lhsT_scale=w1_sc[:, 0, :],
+                rhs=first_codes[:].bitcast(FP8X4),
+                rhs_scale=first_sc[:],
+                start=True,
+                stop=True,
+            )
+        for g in range(GROUPS):
+            w1_pass(0, g)
+        for g in range(2):
+            w1_pass(1, g)
         prepare_w2(0, [(0, HALF_H), (HALF_H, H)])
         for t in range(PACK):
             for g in range(GROUPS):
@@ -193,8 +209,7 @@ def tile_picked_lora_none_e_kernel(
             for t in range(PACK):
                 h_pass(1, g, t)
         for g in range(2, GROUPS):
-            for z in reversed(range(PASSES)):
-                w1_pass(z, g)
+            w1_pass(1, g)
 
         h_bf = []
         for g in range(GROUPS):

@@ -185,16 +185,6 @@ def tile_picked_lora_none_e_kernel(
             for lo, hi in halves if z == 0 else halves[:1]:
                 quantize_x(z, lo, hi, picked[:, lo:hi, :], "x_codes_%d_%d" % (z, lo))
 
-        for g in range(2):
-            nc.tensor.matmul_mx(
-                out=h_acc[g][:].rearrange("p t n -> p (t n)"),
-                lhsT=w1_codes[:, 0, :].bitcast(FP4X4),
-                lhsT_scale=w1_sc[:, 0, :],
-                rhs=first_codes[:].bitcast(FP8X4),
-                rhs_scale=first_sc[:],
-                start=True,
-                stop=True,
-            )
         for g in range(GROUPS):
             w1_pass(0, g)
         for g in range(2):

@@ -21,17 +21,13 @@ PASSES = K // K_PASS
 GROUP = 128
 GROUPS = S // GROUP
 HALF_S = S // 2
-HALF_H = H // 2
 X_PIECES = {
     (0, 0): [(0, 512, 512), (512, 1024, 688)],
     (0, 1): [(0, 512, 512), (512, 1024, 688)],
-    (1, 0): [(0, 512, 512), (512, 1024, 896)],
-    (1, 1): [(0, 512, 512), (512, 1024, 720)],
+    (1, 0): [(0, 512, 512), (512, 1024, 1024)],
+    (1, 1): [(0, 512, 512), (512, 1024, 688)],
 }
-W2_PIECES = [
-    [(0, 256, 256), (256, 512, 432)],
-    [(0, 256, 160), (256, 384, 320), (384, 512, 432)],
-]
+W2_SCALAR = [240, 256]
 
 
 def tile_picked_lora_none_e_kernel(
@@ -40,6 +36,7 @@ def tile_picked_lora_none_e_kernel(
     nc = tc.nc
     with ExitStack() as ctx:
         sb = ctx.enter_context(tc.tile_pool(name="sb", bufs=1))
+        shared = ctx.enter_context(tc.tile_pool(name="shared", bufs=1))
         psum = ctx.enter_context(tc.psum_pool(name="psum", bufs=1))
 
         offsets = sb.tile([P, S // 16], U16, name="offsets")
@@ -51,34 +48,33 @@ def tile_picked_lora_none_e_kernel(
         nc.vector.memset(w3_sc[:].bitcast(I32), 0)
 
         x_rows = xT.rearrange("(z p u e) t -> z u p e t", z=PASSES, p=P, u=2, e=2)
-        w2_rows = w2.rearrange("(z p j) i -> z p j i", z=PASSES, p=P, j=PACK)
+        w2_rows = w2.rearrange("(z p j) i -> z p (j i)", z=PASSES, p=P, j=PACK)
         x_raw, w2_raw = {}, {}
 
         def load_x(z, u):
             for lo, hi, cut in X_PIECES[z, u]:
-                x_raw[z, u, lo] = sb.tile([P, 2, hi - lo], F32, name="x_raw_%d_%d_%d" % (z, u, lo), align_bytes=256)
+                name = "x_raw_%d_%d_%d" % (z, u, lo)
+                x_raw[z, u, lo] = sb.tile([P, 2, hi - lo], F32, name=name, tag=name, align_bytes=256)
                 nc.sync.dma_start(out=x_raw[z, u, lo][:], in_=x_rows[z, u][:, :, lo:hi])
 
-        def load_w2(z, pieces):
-            for lo, hi, cut in pieces:
-                name = "w2_raw_%d_%d" % (z, lo)
-                w2_raw[z, lo] = sb.tile([P, PACK, hi - lo], F32, name=name, tag=name, align_bytes=256)
-                nc.sync.dma_start(out=w2_raw[z, lo][:], in_=w2_rows[z][:, :, lo:hi])
+        def load_w2(z):
+            name = "w2_raw_%d" % z
+            w2_raw[z] = shared.tile([P, PACK * H], F32, name=name, align_bytes=256, offset=(1 - z) * 4 * PACK * H)
+            nc.sync.dma_start(out=w2_raw[z][:], in_=w2_rows[z])
 
         load_x(0, 0)
         nc.sync.dma_start(offsets[:], offs)
         load_x(0, 1)
+        load_x(1, 0)
+        load_w2(0)
+        load_x(1, 1)
+        load_w2(1)
+        nc.sync.dma_start(out=w1_codes[:].bitcast(I32), in_=w1_words.rearrange("z p c -> p z c").bitcast(I32))
         for q in range(4):
             nc.sync.dma_start(
                 out=w1_sc[32 * q : 32 * q + 4, :, :].bitcast(I32),
                 in_=w1_scales[:, 4 * q : 4 * q + 4, :].rearrange("z r c -> r z c").bitcast(I32),
             )
-        load_x(1, 0)
-        load_w2(0, W2_PIECES[0][:0])
-        load_x(1, 1)
-        load_w2(0, W2_PIECES[0][0:])
-        nc.sync.dma_start(out=w1_codes[:].bitcast(I32), in_=w1_words.rearrange("z p c -> p z c").bitcast(I32))
-        load_w2(1, W2_PIECES[1])
         nc.sync.dma_start(out=w3_codes[:].bitcast(I32), in_=w3_words[0].bitcast(I32))
         for q in range(4):
             nc.sync.dma_start(
@@ -89,7 +85,8 @@ def tile_picked_lora_none_e_kernel(
             nc.vector.quantize_mx(out=codes.bitcast(FP8X4), scales=sc, in_=values)
 
         def round_pairs(z, u):
-            pairs = sb.tile([P, T, 2], BF16, name="pairs_%d_%d" % (z, u), align_bytes=64)
+            name = "pairs_%d_%d" % (z, u)
+            pairs = sb.tile([P, T, 2], BF16, name=name, tag=name, align_bytes=256)
             for lo, hi, cut in X_PIECES[z, u]:
                 for copy, a, b in ((nc.scalar.copy, lo, cut), (nc.vector.tensor_copy, cut, hi)):
                     if a < b:
@@ -99,50 +96,46 @@ def tile_picked_lora_none_e_kernel(
         def gather(dst, window, lo, hi):
             nc.vector.tensor_copy(out=dst, in_=window.indirect(offsets[:, lo // 16 : hi // 16]))
 
-        x_codes, x_sc = {}, {}
-        first_codes = sb.tile([P, S], U32, name="first_codes", align_bytes=256)
-        first_sc = sb.tile([P, S], U8, name="first_sc", align_bytes=64)
+        def weave(copy, dst, gathered, lo, hi):
+            copy(out=dst, in_=gathered[:, :, lo:hi].rearrange("p u s -> p s u"))
 
-        def quantize_x(z, lo, hi, words, tag):
-            if z == 0:
-                codes, sc = first_codes[:, lo:hi], first_sc[:, lo:hi]
-            else:
-                codes = sb.tile([P, hi - lo], U32, name="x_codes_%d_%d" % (z, lo), tag=tag, align_bytes=256)[:]
-                sc = sb.tile([P, hi - lo], U8, name="x_sc_%d_%d" % (z, lo), align_bytes=64)[:]
-            quantize(codes, sc, words.rearrange("p s u -> p (s u)").bitcast(BF16))
+        def weave_on_vector(out, in_):
+            nc.vector.tensor_copy(out=out.bitcast(I32), in_=in_.bitcast(I32))
+
+        x_codes, x_sc = {}, {}
+
+        def quantize_x(z, lo, hi, words, codes=None):
+            if codes is None:
+                codes = sb.tile([P, hi - lo], U32, name="x_codes_%d_%d" % (z, lo), align_bytes=256)[:]
+            sc = sb.tile([P, hi - lo], U8, name="x_sc_%d_%d" % (z, lo), align_bytes=64)
+            quantize(codes, sc[:], words.rearrange("p s u -> p (s u)").bitcast(BF16))
             for g in range(lo // GROUP, hi // GROUP):
                 cols = slice(g * GROUP - lo, (g + 1) * GROUP - lo)
                 x_codes[z, g] = codes[:, cols]
                 x_sc[z, g] = sc[:, cols]
 
+        def round_w2(z):
+            grouped = sb.tile([P, PACK, P, PACK], BF16, name="w2_grouped_%d" % z, align_bytes=64)
+            dst = grouped[:].rearrange("p t m j -> p m j t")
+            src = w2_raw[z][:].rearrange("p (j m t) -> p m j t", j=PACK, t=PACK)
+            cut = W2_SCALAR[z] // PACK
+            nc.scalar.copy(out=dst[:, :cut], in_=src[:, :cut])
+            nc.vector.tensor_copy(out=dst[:, cut:], in_=src[:, cut:])
+            return grouped
+
         w2_codes, w2_sc = {}, {}
 
-        def prepare_w2(z, spans):
-            codes = sb.tile([P, PACK, P], U32, name="w2_codes_%d" % z, align_bytes=64)
-            sc = sb.tile([P, PACK, P], U8, name="w2_sc_%d" % z, align_bytes=64)
-            for t in range(PACK):
-                w2_codes[z, t] = codes[:, t, :]
-                w2_sc[z, t] = sc[:, t, :]
-            for c0, c1 in spans:
-                name = "w2_grouped_%d_%d" % (z, c0)
-                grouped = sb.tile([P, PACK, (c1 - c0) // PACK, PACK], BF16, name=name, tag=name, align_bytes=64)
-                for lo, hi, cut in W2_PIECES[z]:
-                    for copy, a, b in ((nc.scalar.copy, lo, cut), (nc.vector.tensor_copy, cut, hi)):
-                        if c0 <= a < b <= c1:
-                            copy(
-                                out=grouped[:, :, (a - c0) // PACK : (b - c0) // PACK, :].rearrange("p t m j -> p m j t"),
-                                in_=w2_raw[z, lo][:, :, a - lo : b - lo].rearrange("p j (m t) -> p m j t", t=PACK),
-                            )
-                if c1 - c0 == H:
-                    quantize(
-                        codes[:].rearrange("p t m -> p (t m)"),
-                        sc[:].rearrange("p t m -> p (t m)"),
-                        grouped[:].rearrange("p t m j -> p (t m j)"),
-                    )
-                else:
-                    cols = slice(c0 // PACK, c1 // PACK)
-                    for t in range(PACK):
-                        quantize(codes[:, t, cols], sc[:, t, cols], grouped[:, t, :, :].rearrange("p m j -> p (m j)"))
+        def quantize_w2(z, grouped, t0, t1, tag):
+            codes = sb.tile([P, t1 - t0, P], U32, name="w2_codes_%d_%d" % (z, t0), tag=tag, align_bytes=256)
+            sc = sb.tile([P, t1 - t0, P], U8, name="w2_sc_%d_%d" % (z, t0), align_bytes=64)
+            quantize(
+                codes[:].rearrange("p t m -> p (t m)"),
+                sc[:].rearrange("p t m -> p (t m)"),
+                grouped[:, t0:t1].rearrange("p t m j -> p (t m j)"),
+            )
+            for t in range(t0, t1):
+                w2_codes[z, t] = codes[:, t - t0, :]
+                w2_sc[z, t] = sc[:, t - t0, :]
 
         h_acc = [psum.tile([P, PACK, GROUP], F32, name="h_acc_%d" % g) for g in range(GROUPS)]
         out_acc = [psum.tile([P, GROUP], F32, name="out_acc_%d" % g) for g in range(GROUPS)]
@@ -170,42 +163,54 @@ def tile_picked_lora_none_e_kernel(
             )
 
         halves = [(0, HALF_S), (HALF_S, S)]
-        for z in range(PASSES):
-            gathered = sb.tile([P, 2, S], U32, name="gathered_%d" % z, align_bytes=64)
-            picked = sb.tile([P, S, 2], U32, name="picked_%d" % z, align_bytes=64)
-            gather(gathered[:, 0, :], round_pairs(z, 0), 0, S)
-            window = round_pairs(z, 1)
-            for lo, hi in halves:
-                gather(gathered[:, 1, lo:hi], window, lo, hi)
-            for lo, hi in halves:
-                nc.vector.tensor_copy(
-                    out=picked[:, lo:hi, :].bitcast(I32),
-                    in_=gathered[:, :, lo:hi].bitcast(I32).rearrange("p u s -> p s u"),
-                )
-            for lo, hi in halves if z == 0 else halves[:1]:
-                quantize_x(z, lo, hi, picked[:, lo:hi, :], "x_codes_%d_%d" % (z, lo))
+        gathered = [sb.tile([P, 2, S], U32, name="gathered_%d" % z, align_bytes=64) for z in range(PASSES)]
 
-        for g in range(GROUPS):
-            w1_pass(0, g)
-        for g in range(2):
-            w1_pass(1, g)
-        prepare_w2(0, [(0, HALF_H), (HALF_H, H)])
+        gather(gathered[0][:, 0, :], round_pairs(0, 0), 0, S)
+        window = round_pairs(0, 1)
+        first = sb.tile([P, S, 2], U32, name="picked_first", align_bytes=64)
+        for lo, hi in halves:
+            gather(gathered[0][:, 1, lo:hi], window, lo, hi)
+        for lo, hi in halves:
+            weave(weave_on_vector, first[:, lo:hi, :], gathered[0], lo, hi)
+        for lo, hi in halves:
+            quantize_x(0, lo, hi, first[:, lo:hi, :])
+        gather(gathered[1][:, 0, :], round_pairs(1, 0), 0, S)
+        grouped = round_w2(0)
+
+        window = round_pairs(1, 1)
+        quantize_w2(0, grouped, 0, 2, "x_raw_1_1_0")
+        early = sb.tile([P, HALF_S, 2], U32, name="picked_early", align_bytes=64)
+        for lo in (0, GROUP):
+            gather(gathered[1][:, 1, lo : lo + GROUP], window, lo, lo + GROUP)
+            weave(nc.scalar.copy, early[:, lo : lo + GROUP, :], gathered[1], lo, lo + GROUP)
+        gather(gathered[1][:, 1, HALF_S:], window, HALF_S, S)
+        quantize_w2(0, grouped, 2, PACK, "x_raw_1_1_512")
+        quantize_x(1, 0, HALF_S, early[:])
         for t in range(PACK):
             for g in range(GROUPS):
                 h_pass(0, g, t)
-        prepare_w2(1, [(0, HALF_H), (HALF_H, H)])
-        quantize_x(1, HALF_S, S, picked[:, HALF_S:, :], "w2_raw_1_%d" % W2_PIECES[1][-1][0])
-        for g in range(GROUPS):
-            for t in range(PACK):
+
+        grouped = round_w2(1)
+        late = shared.tile([P, HALF_S, 2], U32, name="picked_late", align_bytes=256, offset=4 * HALF_S)
+        weave(nc.scalar.copy, late[:], gathered[1], HALF_S, S)
+        for t in range(PACK):
+            quantize_w2(1, grouped, t, t + 1, "w2_codes_1_%d" % t)
+        quantize_x(1, HALF_S, S, late[:])
+        for t in range(PACK):
+            for g in range(2):
                 h_pass(1, g, t)
         for g in range(2, GROUPS):
-            w1_pass(1, g)
+            for t in range(PACK):
+                h_pass(1, g, t)
+        for g in range(GROUPS):
+            for z in range(PASSES):
+                w1_pass(z, g)
 
         h_bf = []
         for g in range(GROUPS):
             hb = sb.tile([P, GROUP, PACK], BF16, name="h_bf_%d" % g, align_bytes=64)
             h_bf.append(hb)
-            copy = nc.vector.tensor_copy if g % 2 == 0 else nc.scalar.copy
+            copy = nc.scalar.copy if g in (0, GROUPS - 1) else nc.vector.tensor_copy
             copy(out=hb[:], in_=h_acc[g][:].rearrange("p t n -> p n t"))
 
         for g in range(GROUPS):

@@ -21,13 +21,17 @@ PASSES = K // K_PASS
 GROUP = 128
 GROUPS = S // GROUP
 HALF_S = S // 2
+HALF_P = P // 2
 X_PIECES = {
     (0, 0): [(0, 512, 512), (512, 1024, 688)],
     (0, 1): [(0, 512, 512), (512, 1024, 688)],
-    (1, 0): [(0, 512, 512), (512, 1024, 1024)],
-    (1, 1): [(0, 512, 512), (512, 1024, 688)],
+    (1, 0): [(0, 512, 512), (512, 1024, 896)],
+    (1, 1): [(0, 512, 512), (512, 1024, 752)],
 }
-W2_SCALAR = [240, 256]
+W2_PIECES = [
+    [(0, 256, 256), (256, 512, 336)],
+    [(0, 256, 256), (256, 384, 256), (384, 512, 464)],
+]
 
 
 def tile_picked_lora_none_e_kernel(
@@ -36,7 +40,6 @@ def tile_picked_lora_none_e_kernel(
     nc = tc.nc
     with ExitStack() as ctx:
         sb = ctx.enter_context(tc.tile_pool(name="sb", bufs=1))
-        shared = ctx.enter_context(tc.tile_pool(name="shared", bufs=1))
         psum = ctx.enter_context(tc.psum_pool(name="psum", bufs=1))
 
         offsets = sb.tile([P, S // 16], U16, name="offsets")
@@ -48,7 +51,7 @@ def tile_picked_lora_none_e_kernel(
         nc.vector.memset(w3_sc[:].bitcast(I32), 0)
 
         x_rows = xT.rearrange("(z p u e) t -> z u p e t", z=PASSES, p=P, u=2, e=2)
-        w2_rows = w2.rearrange("(z p j) i -> z p (j i)", z=PASSES, p=P, j=PACK)
+        w2_rows = w2.rearrange("(z p j) i -> z p j i", z=PASSES, p=P, j=PACK)
         x_raw, w2_raw = {}, {}
 
         def load_x(z, u):
@@ -58,16 +61,17 @@ def tile_picked_lora_none_e_kernel(
                 nc.sync.dma_start(out=x_raw[z, u, lo][:], in_=x_rows[z, u][:, :, lo:hi])
 
         def load_w2(z):
-            name = "w2_raw_%d" % z
-            w2_raw[z] = shared.tile([P, PACK * H], F32, name=name, align_bytes=256, offset=(1 - z) * 4 * PACK * H)
-            nc.sync.dma_start(out=w2_raw[z][:], in_=w2_rows[z])
+            for lo, hi, cut in W2_PIECES[z]:
+                name = "w2_raw_%d_%d" % (z, lo)
+                w2_raw[z, lo] = sb.tile([P, PACK, hi - lo], F32, name=name, tag=name, align_bytes=256)
+                nc.sync.dma_start(out=w2_raw[z, lo][:], in_=w2_rows[z][:, :, lo:hi])
 
         load_x(0, 0)
         nc.sync.dma_start(offsets[:], offs)
         load_x(0, 1)
         load_x(1, 0)
-        load_w2(0)
         load_x(1, 1)
+        load_w2(0)
         load_w2(1)
         nc.sync.dma_start(out=w1_codes[:].bitcast(I32), in_=w1_words.rearrange("z p c -> p z c").bitcast(I32))
         for q in range(4):
@@ -104,38 +108,40 @@ def tile_picked_lora_none_e_kernel(
 
         x_codes, x_sc = {}, {}
 
-        def quantize_x(z, lo, hi, words, codes=None):
-            if codes is None:
-                codes = sb.tile([P, hi - lo], U32, name="x_codes_%d_%d" % (z, lo), align_bytes=256)[:]
+        def quantize_x(z, lo, hi, words, tag):
+            codes = sb.tile([P, hi - lo], U32, name="x_codes_%d_%d" % (z, lo), tag=tag, align_bytes=256)
             sc = sb.tile([P, hi - lo], U8, name="x_sc_%d_%d" % (z, lo), align_bytes=64)
-            quantize(codes, sc[:], words.rearrange("p s u -> p (s u)").bitcast(BF16))
+            quantize(codes[:], sc[:], words.rearrange("p s u -> p (s u)").bitcast(BF16))
             for g in range(lo // GROUP, hi // GROUP):
                 cols = slice(g * GROUP - lo, (g + 1) * GROUP - lo)
                 x_codes[z, g] = codes[:, cols]
                 x_sc[z, g] = sc[:, cols]
 
+        w2_codes = [sb.tile([P, PACK, P], U32, name="w2_codes_%d" % z, align_bytes=64) for z in range(PASSES)]
+        w2_sc = [sb.tile([P, PACK, P], U8, name="w2_sc_%d" % z, align_bytes=64) for z in range(PASSES)]
+
         def round_w2(z):
-            grouped = sb.tile([P, PACK, P, PACK], BF16, name="w2_grouped_%d" % z, align_bytes=64)
-            dst = grouped[:].rearrange("p t m j -> p m j t")
-            src = w2_raw[z][:].rearrange("p (j m t) -> p m j t", j=PACK, t=PACK)
-            cut = W2_SCALAR[z] // PACK
-            nc.scalar.copy(out=dst[:, :cut], in_=src[:, :cut])
-            nc.vector.tensor_copy(out=dst[:, cut:], in_=src[:, cut:])
+            grouped = [
+                sb.tile([P, PACK, HALF_P, PACK], BF16, name="w2_grouped_%d_%d" % (z, half), align_bytes=64)
+                for half in range(2)
+            ]
+            for lo, hi, cut in W2_PIECES[z]:
+                half, c0 = lo // (H // 2), lo // (H // 2) * (H // 2)
+                for copy, a, b in ((nc.scalar.copy, lo, cut), (nc.vector.tensor_copy, cut, hi)):
+                    if a < b:
+                        copy(
+                            out=grouped[half][:, :, (a - c0) // PACK : (b - c0) // PACK, :].rearrange("p t m j -> p m j t"),
+                            in_=w2_raw[z, lo][:, :, a - lo : b - lo].rearrange("p j (m t) -> p m j t", t=PACK),
+                        )
             return grouped
 
-        w2_codes, w2_sc = {}, {}
-
-        def quantize_w2(z, grouped, t0, t1, tag):
-            codes = sb.tile([P, t1 - t0, P], U32, name="w2_codes_%d_%d" % (z, t0), tag=tag, align_bytes=256)
-            sc = sb.tile([P, t1 - t0, P], U8, name="w2_sc_%d_%d" % (z, t0), align_bytes=64)
-            quantize(
-                codes[:].rearrange("p t m -> p (t m)"),
-                sc[:].rearrange("p t m -> p (t m)"),
-                grouped[:, t0:t1].rearrange("p t m j -> p (t m j)"),
-            )
-            for t in range(t0, t1):
-                w2_codes[z, t] = codes[:, t - t0, :]
-                w2_sc[z, t] = sc[:, t - t0, :]
+        def quantize_w2(z, grouped):
+            for half in range(2):
+                cols = slice(half * HALF_P, (half + 1) * HALF_P)
+                for t in range(PACK):
+                    quantize(
+                        w2_codes[z][:, t, cols], w2_sc[z][:, t, cols], grouped[half][:, t, :, :].rearrange("p m j -> p (m j)")
+                    )
 
         h_acc = [psum.tile([P, PACK, GROUP], F32, name="h_acc_%d" % g) for g in range(GROUPS)]
         out_acc = [psum.tile([P, GROUP], F32, name="out_acc_%d" % g) for g in range(GROUPS)]
@@ -143,8 +149,8 @@ def tile_picked_lora_none_e_kernel(
         def h_pass(z, g, t):
             nc.tensor.matmul_mx(
                 out=h_acc[g][:, t, :],
-                lhsT=w2_codes[z, t].bitcast(FP8X4),
-                lhsT_scale=w2_sc[z, t],
+                lhsT=w2_codes[z][:, t, :].bitcast(FP8X4),
+                lhsT_scale=w2_sc[z][:, t, :],
                 rhs=x_codes[z, g].bitcast(FP8X4),
                 rhs_scale=x_sc[z, g],
                 start=(z == 0 and t == 0),
@@ -172,34 +178,27 @@ def tile_picked_lora_none_e_kernel(
             gather(gathered[0][:, 1, lo:hi], window, lo, hi)
         for lo, hi in halves:
             weave(weave_on_vector, first[:, lo:hi, :], gathered[0], lo, hi)
-        for lo, hi in halves:
-            quantize_x(0, lo, hi, first[:, lo:hi, :])
+        quantize_x(0, 0, HALF_S, first[:, :HALF_S, :], "x_codes_0_0")
         gather(gathered[1][:, 0, :], round_pairs(1, 0), 0, S)
-        grouped = round_w2(0)
-
         window = round_pairs(1, 1)
-        quantize_w2(0, grouped, 0, 2, "x_raw_1_1_0")
-        early = sb.tile([P, HALF_S, 2], U32, name="picked_early", align_bytes=64)
-        for lo in (0, GROUP):
-            gather(gathered[1][:, 1, lo : lo + GROUP], window, lo, lo + GROUP)
-            weave(nc.scalar.copy, early[:, lo : lo + GROUP, :], gathered[1], lo, lo + GROUP)
-        gather(gathered[1][:, 1, HALF_S:], window, HALF_S, S)
-        quantize_w2(0, grouped, 2, PACK, "x_raw_1_1_512")
-        quantize_x(1, 0, HALF_S, early[:])
+        quantize_x(0, HALF_S, S, first[:, HALF_S:, :], "x_raw_1_1_0")
+        for lo, hi in halves:
+            gather(gathered[1][:, 1, lo:hi], window, lo, hi)
+
+        quantize_w2(0, round_w2(0))
         for t in range(PACK):
             for g in range(GROUPS):
                 h_pass(0, g, t)
 
+        early = sb.tile([P, HALF_S, 2], U32, name="picked_early", tag="w2_raw_0_0", align_bytes=256)
+        late = sb.tile([P, HALF_S, 2], U32, name="picked_late", tag="w2_raw_0_256", align_bytes=256)
+        weave(nc.scalar.copy, early[:], gathered[1], 0, HALF_S)
+        weave(weave_on_vector, late[:], gathered[1], HALF_S, S)
+        quantize_x(1, 0, HALF_S, early[:], "x_codes_1_0")
         grouped = round_w2(1)
-        late = shared.tile([P, HALF_S, 2], U32, name="picked_late", align_bytes=256, offset=4 * HALF_S)
-        weave(nc.scalar.copy, late[:], gathered[1], HALF_S, S)
-        for t in range(PACK):
-            quantize_w2(1, grouped, t, t + 1, "w2_codes_1_%d" % t)
-        quantize_x(1, HALF_S, S, late[:])
-        for t in range(PACK):
-            for g in range(2):
-                h_pass(1, g, t)
-        for g in range(2, GROUPS):
+        quantize_x(1, HALF_S, S, late[:], "x_codes_1_256")
+        quantize_w2(1, grouped)
+        for g in range(GROUPS):
             for t in range(PACK):
                 h_pass(1, g, t)
         for g in range(GROUPS):
@@ -210,7 +209,7 @@ def tile_picked_lora_none_e_kernel(
         for g in range(GROUPS):
             hb = sb.tile([P, GROUP, PACK], BF16, name="h_bf_%d" % g, align_bytes=64)
             h_bf.append(hb)
-            copy = nc.scalar.copy if g in (0, GROUPS - 1) else nc.vector.tensor_copy
+            copy = nc.vector.tensor_copy if g % 2 == 0 else nc.scalar.copy
             copy(out=hb[:], in_=h_acc[g][:].rearrange("p t n -> p n t"))
 
         for g in range(GROUPS):

@@ -25,8 +25,8 @@ HALF_P = P // 2
 X_PIECES = {
     (0, 0): [(0, 512, 512), (512, 1024, 688)],
     (0, 1): [(0, 512, 512), (512, 1024, 688)],
-    (1, 0): [(0, 512, 512), (512, 1024, 896)],
-    (1, 1): [(0, 512, 512), (512, 1024, 752)],
+    (1, 0): [(0, 512, 512), (512, 1024, 704)],
+    (1, 1): [(0, 512, 512), (512, 1024, 688)],
 }
 W2_PIECES = [
     [(0, 256, 256), (256, 512, 336)],
@@ -40,6 +40,7 @@ def tile_picked_lora_none_e_kernel(
     nc = tc.nc
     with ExitStack() as ctx:
         sb = ctx.enter_context(tc.tile_pool(name="sb", bufs=1))
+        shared = ctx.enter_context(tc.tile_pool(name="shared", bufs=1))
         psum = ctx.enter_context(tc.psum_pool(name="psum", bufs=1))
 
         offsets = sb.tile([P, S // 16], U16, name="offsets")
@@ -57,7 +58,10 @@ def tile_picked_lora_none_e_kernel(
         def load_x(z, u):
             for lo, hi, cut in X_PIECES[z, u]:
                 name = "x_raw_%d_%d_%d" % (z, u, lo)
-                x_raw[z, u, lo] = sb.tile([P, 2, hi - lo], F32, name=name, tag=name, align_bytes=256)
+                if (z, u, lo) == (1, 0, 0):
+                    x_raw[z, u, lo] = shared.tile([P, 2, hi - lo], F32, name=name, align_bytes=256, offset=0)
+                else:
+                    x_raw[z, u, lo] = sb.tile([P, 2, hi - lo], F32, name=name, tag=name, align_bytes=256)
                 nc.sync.dma_start(out=x_raw[z, u, lo][:], in_=x_rows[z, u][:, :, lo:hi])
 
         def load_w2(z):
@@ -109,7 +113,10 @@ def tile_picked_lora_none_e_kernel(
         x_codes, x_sc = {}, {}
 
         def quantize_x(z, lo, hi, words, tag):
-            codes = sb.tile([P, hi - lo], U32, name="x_codes_%d_%d" % (z, lo), tag=tag, align_bytes=256)
+            if tag is None:
+                codes = shared.tile([P, hi - lo], U32, name="x_codes_%d_%d" % (z, lo), align_bytes=256, offset=0)
+            else:
+                codes = sb.tile([P, hi - lo], U32, name="x_codes_%d_%d" % (z, lo), tag=tag, align_bytes=256)
             sc = sb.tile([P, hi - lo], U8, name="x_sc_%d_%d" % (z, lo), align_bytes=64)
             quantize(codes[:], sc[:], words.rearrange("p s u -> p (s u)").bitcast(BF16))
             for g in range(lo // GROUP, hi // GROUP):
@@ -173,15 +180,17 @@ def tile_picked_lora_none_e_kernel(
 
         gather(gathered[0][:, 0, :], round_pairs(0, 0), 0, S)
         window = round_pairs(0, 1)
-        first = sb.tile([P, S, 2], U32, name="picked_first", align_bytes=64)
+        first = sb.tile([P, HALF_S, 2], U32, name="picked_first", align_bytes=64)
+        second = shared.tile([P, HALF_S, 2], U32, name="picked_second", align_bytes=256, offset=4 * HALF_S)
         for lo, hi in halves:
             gather(gathered[0][:, 1, lo:hi], window, lo, hi)
-        for lo, hi in halves:
-            weave(weave_on_vector, first[:, lo:hi, :], gathered[0], lo, hi)
-        quantize_x(0, 0, HALF_S, first[:, :HALF_S, :], "x_codes_0_0")
-        gather(gathered[1][:, 0, :], round_pairs(1, 0), 0, S)
+        weave(weave_on_vector, first[:], gathered[0], 0, HALF_S)
+        window = round_pairs(1, 0)
+        weave(nc.scalar.copy, second[:], gathered[0], HALF_S, S)
+        quantize_x(0, 0, HALF_S, first[:], None)
+        gather(gathered[1][:, 0, :], window, 0, S)
         window = round_pairs(1, 1)
-        quantize_x(0, HALF_S, S, first[:, HALF_S:, :], "x_raw_1_1_0")
+        quantize_x(0, HALF_S, S, second[:], "x_raw_1_1_0")
         for lo, hi in halves:
             gather(gathered[1][:, 1, lo:hi], window, lo, hi)
 

@@ -23,9 +23,9 @@ GROUPS = S // GROUP
 HALF_S = S // 2
 HALF_P = P // 2
 X_PIECES = {
-    (0, 0): [(0, 512, 512), (512, 1024, 688)],
-    (0, 1): [(0, 512, 512), (512, 1024, 688)],
-    (1, 0): [(0, 512, 512), (512, 1024, 704)],
+    (0, 0): [(0, 1024, 384)],
+    (0, 1): [(0, 1024, 384)],
+    (1, 0): [(0, 512, 512), (512, 1024, 848)],
     (1, 1): [(0, 512, 512), (512, 1024, 688)],
 }
 W2_PIECES = [

@@ -13,25 +13,16 @@ U16 = mybir.dt.uint16
 U8 = mybir.dt.uint8
 FP8X4 = mybir.dt.float8_e4m3fn_x4
 FP4X4 = mybir.dt.float4_e2m1fn_x4
+COPY = mybir.ActivationFunctionType.Copy
 
 P = 128
 PACK = 4
-K_PASS = P * PACK
-PASSES = K // K_PASS
+PASSES = K // (P * PACK)
 GROUP = 128
 GROUPS = S // GROUP
 HALF_S = S // 2
-HALF_P = P // 2
-X_PIECES = {
-    (0, 0): [(0, 1024, 384)],
-    (0, 1): [(0, 1024, 384)],
-    (1, 0): [(0, 512, 512), (512, 1024, 848)],
-    (1, 1): [(0, 512, 512), (512, 1024, 688)],
-}
-W2_PIECES = [
-    [(0, 256, 256), (256, 512, 336)],
-    [(0, 256, 256), (256, 384, 256), (384, 512, 464)],
-]
+X_LOADS = [(0, 0, 2), (0, 2, 4), (1, 0, 2), (1, 2, 3), (1, 3, 4)]
+W2_CUT = 88
 
 
 def tile_picked_lora_none_e_kernel(
@@ -40,7 +31,6 @@ def tile_picked_lora_none_e_kernel(
     nc = tc.nc
     with ExitStack() as ctx:
         sb = ctx.enter_context(tc.tile_pool(name="sb", bufs=1))
-        shared = ctx.enter_context(tc.tile_pool(name="shared", bufs=1))
         psum = ctx.enter_context(tc.psum_pool(name="psum", bufs=1))
 
         offsets = sb.tile([P, S // 16], U16, name="offsets")
@@ -49,34 +39,20 @@ def tile_picked_lora_none_e_kernel(
         w1_sc = sb.tile([P, PASSES, N], U8, name="w1_sc", align_bytes=64)
         w3_sc = sb.tile([P, N], U8, name="w3_sc", align_bytes=64)
         nc.vector.memset(w1_sc[:].bitcast(I32), 0)
-        nc.vector.memset(w3_sc[:].bitcast(I32), 0)
+        nc.scalar.copy(out=w3_sc[:].bitcast(U32), in_=w1_sc[:, 0, :].bitcast(U32))
 
-        x_rows = xT.rearrange("(z p u e) t -> z u p e t", z=PASSES, p=P, u=2, e=2)
+        x_rows = xT.rearrange("(z p j) t -> z p (j t)", z=PASSES, p=P, j=PACK)
         w2_rows = w2.rearrange("(z p j) i -> z p j i", z=PASSES, p=P, j=PACK)
         x_raw, w2_raw = {}, {}
 
-        def load_x(z, u):
-            for lo, hi, cut in X_PIECES[z, u]:
-                name = "x_raw_%d_%d_%d" % (z, u, lo)
-                if (z, u, lo) == (1, 0, 0):
-                    x_raw[z, u, lo] = shared.tile([P, 2, hi - lo], F32, name=name, align_bytes=256, offset=0)
-                else:
-                    x_raw[z, u, lo] = sb.tile([P, 2, hi - lo], F32, name=name, tag=name, align_bytes=256)
-                nc.sync.dma_start(out=x_raw[z, u, lo][:], in_=x_rows[z, u][:, :, lo:hi])
-
-        def load_w2(z):
-            for lo, hi, cut in W2_PIECES[z]:
-                name = "w2_raw_%d_%d" % (z, lo)
-                w2_raw[z, lo] = sb.tile([P, PACK, hi - lo], F32, name=name, tag=name, align_bytes=256)
-                nc.sync.dma_start(out=w2_raw[z, lo][:], in_=w2_rows[z][:, :, lo:hi])
-
-        load_x(0, 0)
-        nc.sync.dma_start(offsets[:], offs)
-        load_x(0, 1)
-        load_x(1, 0)
-        load_x(1, 1)
-        load_w2(0)
-        load_w2(1)
+        for z, j0, j1 in X_LOADS:
+            x_raw[z, j0] = sb.tile([P, (j1 - j0) * T], F32, name="x_raw_%d_%d" % (z, j0), align_bytes=256)
+            nc.sync.dma_start(out=x_raw[z, j0][:], in_=x_rows[z][:, j0 * T : j1 * T])
+            if (z, j0) == (0, 0):
+                nc.sync.dma_start(offsets[:], offs)
+        for z in range(PASSES):
+            w2_raw[z] = sb.tile([P, PACK, H], F32, name="w2_raw_%d" % z, align_bytes=256)
+            nc.sync.dma_start(out=w2_raw[z][:], in_=w2_rows[z])
         nc.sync.dma_start(out=w1_codes[:].bitcast(I32), in_=w1_words.rearrange("z p c -> p z c").bitcast(I32))
         for q in range(4):
             nc.sync.dma_start(
@@ -92,64 +68,30 @@ def tile_picked_lora_none_e_kernel(
         def quantize(codes, sc, values):
             nc.vector.quantize_mx(out=codes.bitcast(FP8X4), scales=sc, in_=values)
 
-        def round_pairs(z, u):
-            name = "pairs_%d_%d" % (z, u)
-            pairs = sb.tile([P, T, 2], BF16, name=name, tag=name, align_bytes=256)
-            for lo, hi, cut in X_PIECES[z, u]:
-                for copy, a, b in ((nc.scalar.copy, lo, cut), (nc.vector.tensor_copy, cut, hi)):
-                    if a < b:
-                        copy(out=pairs[:, a:b, :], in_=x_raw[z, u, lo][:, :, a - lo : b - lo].rearrange("p e t -> p t e"))
-            return pairs[:].rearrange("p t e -> p (t e)").bitcast(U32)
+        x_codes = [sb.tile([P, S], U32, name="x_codes_%d" % z, align_bytes=64) for z in range(PASSES)]
+        x_sc = [sb.tile([P, S], U8, name="x_sc_%d" % z, align_bytes=64) for z in range(PASSES)]
 
-        def gather(dst, window, lo, hi):
-            nc.vector.tensor_copy(out=dst, in_=window.indirect(offsets[:, lo // 16 : hi // 16]))
+        def group_cols(g):
+            return slice(g * GROUP, (g + 1) * GROUP)
 
-        def weave(copy, dst, gathered, lo, hi):
-            copy(out=dst, in_=gathered[:, :, lo:hi].rearrange("p u s -> p s u"))
-
-        def weave_on_vector(out, in_):
-            nc.vector.tensor_copy(out=out.bitcast(I32), in_=in_.bitcast(I32))
-
-        x_codes, x_sc = {}, {}
-
-        def quantize_x(z, lo, hi, words, tag):
-            if tag is None:
-                codes = shared.tile([P, hi - lo], U32, name="x_codes_%d_%d" % (z, lo), align_bytes=256, offset=0)
-            else:
-                codes = sb.tile([P, hi - lo], U32, name="x_codes_%d_%d" % (z, lo), tag=tag, align_bytes=256)
-            sc = sb.tile([P, hi - lo], U8, name="x_sc_%d_%d" % (z, lo), align_bytes=64)
-            quantize(codes[:], sc[:], words.rearrange("p s u -> p (s u)").bitcast(BF16))
-            for g in range(lo // GROUP, hi // GROUP):
-                cols = slice(g * GROUP - lo, (g + 1) * GROUP - lo)
-                x_codes[z, g] = codes[:, cols]
-                x_sc[z, g] = sc[:, cols]
+        for z in range(PASSES):
+            planes = sb.tile([P, PACK, S], F32, name="planes_%d" % z, align_bytes=64)
+            for j0, j1 in [load[1:] for load in X_LOADS if load[0] == z]:
+                for j in range(j0, j1):
+                    window = x_raw[z, j0][:, (j - j0) * T : (j - j0 + 1) * T]
+                    nc.vector.tensor_copy(out=planes[:, j, :HALF_S], in_=window.indirect(offsets[:, : HALF_S // 16]))
+                    nc.scalar.activation(
+                        out=planes[:, j, HALF_S:], in_=window.indirect(offsets[:, HALF_S // 16 :]), func=COPY
+                    )
+            x_bf = [sb.tile([P, GROUP, PACK], BF16, name="x_bf_%d_%d" % (z, g), align_bytes=64) for g in range(GROUPS)]
+            for g in range(GROUPS):
+                copy = nc.vector.tensor_copy if g < GROUPS // 2 else nc.scalar.copy
+                copy(out=x_bf[g][:], in_=planes[:, :, group_cols(g)].rearrange("p j s -> p s j"))
+            for g in range(GROUPS):
+                quantize(x_codes[z][:, group_cols(g)], x_sc[z][:, group_cols(g)], x_bf[g][:].rearrange("p s j -> p (s j)"))
 
         w2_codes = [sb.tile([P, PACK, P], U32, name="w2_codes_%d" % z, align_bytes=64) for z in range(PASSES)]
         w2_sc = [sb.tile([P, PACK, P], U8, name="w2_sc_%d" % z, align_bytes=64) for z in range(PASSES)]
-
-        def round_w2(z):
-            grouped = [
-                sb.tile([P, PACK, HALF_P, PACK], BF16, name="w2_grouped_%d_%d" % (z, half), align_bytes=64)
-                for half in range(2)
-            ]
-            for lo, hi, cut in W2_PIECES[z]:
-                half, c0 = lo // (H // 2), lo // (H // 2) * (H // 2)
-                for copy, a, b in ((nc.scalar.copy, lo, cut), (nc.vector.tensor_copy, cut, hi)):
-                    if a < b:
-                        copy(
-                            out=grouped[half][:, :, (a - c0) // PACK : (b - c0) // PACK, :].rearrange("p t m j -> p m j t"),
-                            in_=w2_raw[z, lo][:, :, a - lo : b - lo].rearrange("p j (m t) -> p m j t", t=PACK),
-                        )
-            return grouped
-
-        def quantize_w2(z, grouped):
-            for half in range(2):
-                cols = slice(half * HALF_P, (half + 1) * HALF_P)
-                for t in range(PACK):
-                    quantize(
-                        w2_codes[z][:, t, cols], w2_sc[z][:, t, cols], grouped[half][:, t, :, :].rearrange("p m j -> p (m j)")
-                    )
-
         h_acc = [psum.tile([P, PACK, GROUP], F32, name="h_acc_%d" % g) for g in range(GROUPS)]
         out_acc = [psum.tile([P, GROUP], F32, name="out_acc_%d" % g) for g in range(GROUPS)]
 
@@ -158,68 +100,43 @@ def tile_picked_lora_none_e_kernel(
                 out=h_acc[g][:, t, :],
                 lhsT=w2_codes[z][:, t, :].bitcast(FP8X4),
                 lhsT_scale=w2_sc[z][:, t, :],
-                rhs=x_codes[z, g].bitcast(FP8X4),
-                rhs_scale=x_sc[z, g],
+                rhs=x_codes[z][:, group_cols(g)].bitcast(FP8X4),
+                rhs_scale=x_sc[z][:, group_cols(g)],
                 start=(z == 0 and t == 0),
                 stop=(z == PASSES - 1 and t == PACK - 1),
             )
 
-        def w1_pass(z, g):
-            nc.tensor.matmul_mx(
-                out=out_acc[g][:],
-                lhsT=w1_codes[:, z, :].bitcast(FP4X4),
-                lhsT_scale=w1_sc[:, z, :],
-                rhs=x_codes[z, g].bitcast(FP8X4),
-                rhs_scale=x_sc[z, g],
-                start=(z == 0),
-                stop=False,
-            )
-
-        halves = [(0, HALF_S), (HALF_S, S)]
-        gathered = [sb.tile([P, 2, S], U32, name="gathered_%d" % z, align_bytes=64) for z in range(PASSES)]
-
-        gather(gathered[0][:, 0, :], round_pairs(0, 0), 0, S)
-        window = round_pairs(0, 1)
-        first = sb.tile([P, HALF_S, 2], U32, name="picked_first", align_bytes=64)
-        second = shared.tile([P, HALF_S, 2], U32, name="picked_second", align_bytes=256, offset=4 * HALF_S)
-        for lo, hi in halves:
-            gather(gathered[0][:, 1, lo:hi], window, lo, hi)
-        weave(weave_on_vector, first[:], gathered[0], 0, HALF_S)
-        window = round_pairs(1, 0)
-        weave(nc.scalar.copy, second[:], gathered[0], HALF_S, S)
-        quantize_x(0, 0, HALF_S, first[:], None)
-        gather(gathered[1][:, 0, :], window, 0, S)
-        window = round_pairs(1, 1)
-        quantize_x(0, HALF_S, S, second[:], "x_raw_1_1_0")
-        for lo, hi in halves:
-            gather(gathered[1][:, 1, lo:hi], window, lo, hi)
-
-        quantize_w2(0, round_w2(0))
-        for t in range(PACK):
-            for g in range(GROUPS):
-                h_pass(0, g, t)
-
-        early = sb.tile([P, HALF_S, 2], U32, name="picked_early", tag="w2_raw_0_0", align_bytes=256)
-        late = sb.tile([P, HALF_S, 2], U32, name="picked_late", tag="w2_raw_0_256", align_bytes=256)
-        weave(nc.scalar.copy, early[:], gathered[1], 0, HALF_S)
-        weave(weave_on_vector, late[:], gathered[1], HALF_S, S)
-        quantize_x(1, 0, HALF_S, early[:], "x_codes_1_0")
-        grouped = round_w2(1)
-        quantize_x(1, HALF_S, S, late[:], "x_codes_1_256")
-        quantize_w2(1, grouped)
-        for g in range(GROUPS):
+        for z in range(PASSES):
+            dealt = [sb.tile([P, 2, P, PACK], BF16, name="w2_dealt_%d_%d" % (z, v), align_bytes=64) for v in range(2)]
+            raw = w2_raw[z][:].rearrange("p j (m v e) -> p v m j e", v=2, e=2)
+            for copy, v, lo, hi in (
+                (nc.vector.tensor_copy, 0, 0, P),
+                (nc.scalar.copy, 1, 0, W2_CUT),
+                (nc.vector.tensor_copy, 1, W2_CUT, P),
+            ):
+                copy(out=dealt[v][:, :, lo:hi, :].rearrange("p e m j -> p m j e"), in_=raw[:, v, lo:hi])
             for t in range(PACK):
-                h_pass(1, g, t)
+                quantize(w2_codes[z][:, t, :], w2_sc[z][:, t, :], dealt[t // 2][:, t % 2].rearrange("p m j -> p (m j)"))
+            for g0 in range(0, GROUPS, 2):
+                for t in range(PACK):
+                    for g in (g0, g0 + 1):
+                        h_pass(z, g, t)
         for g in range(GROUPS):
             for z in range(PASSES):
-                w1_pass(z, g)
+                nc.tensor.matmul_mx(
+                    out=out_acc[g][:],
+                    lhsT=w1_codes[:, z, :].bitcast(FP4X4),
+                    lhsT_scale=w1_sc[:, z, :],
+                    rhs=x_codes[z][:, group_cols(g)].bitcast(FP8X4),
+                    rhs_scale=x_sc[z][:, group_cols(g)],
+                    start=(z == 0),
+                    stop=False,
+                )
 
-        h_bf = []
+        h_bf = [sb.tile([P, GROUP, PACK], BF16, name="h_bf_%d" % g, align_bytes=64) for g in range(GROUPS)]
         for g in range(GROUPS):
-            hb = sb.tile([P, GROUP, PACK], BF16, name="h_bf_%d" % g, align_bytes=64)
-            h_bf.append(hb)
             copy = nc.vector.tensor_copy if g % 2 == 0 else nc.scalar.copy
-            copy(out=hb[:], in_=h_acc[g][:].rearrange("p t n -> p n t"))
+            copy(out=h_bf[g][:], in_=h_acc[g][:].rearrange("p t n -> p n t"))
 
         for g in range(GROUPS):
             codes = sb.tile([P, GROUP], U32, name="h_codes_%d" % g, align_bytes=64)
@@ -237,4 +154,4 @@ def tile_picked_lora_none_e_kernel(
             res = sb.tile([P, GROUP], F32, name="res_%d" % g, align_bytes=256)
             copy = nc.vector.tensor_copy if g == GROUPS - 1 else nc.scalar.copy
             copy(out=res[:], in_=out_acc[g][:])
-            nc.sync.dma_start(out=out[:, g * GROUP : (g + 1) * GROUP], in_=res[:])
+            nc.sync.dma_start(out=out[:, group_cols(g)], in_=res[:])

@@ -21,8 +21,12 @@ PASSES = K // (P * PACK)
 GROUP = 128
 GROUPS = S // GROUP
 HALF_S = S // 2
-X_LOADS = [(0, 0, 2), (0, 2, 4), (1, 0, 2), (1, 2, 3), (1, 3, 4)]
-W2_CUT = 88
+HALF_P = P // 2
+GATHER_CUT = 192
+W2_PIECES = [
+    [(0, 256, 256), (256, 512, 336)],
+    [(0, 256, 168), (256, 384, 336), (384, 512, 448)],
+]
 
 
 def tile_picked_lora_none_e_kernel(
@@ -43,16 +47,26 @@ def tile_picked_lora_none_e_kernel(
 
         x_rows = xT.rearrange("(z p j) t -> z p (j t)", z=PASSES, p=P, j=PACK)
         w2_rows = w2.rearrange("(z p j) i -> z p j i", z=PASSES, p=P, j=PACK)
-        x_raw, w2_raw = {}, {}
+        windows, w2_raw = {}, {}
 
-        for z, j0, j1 in X_LOADS:
-            x_raw[z, j0] = sb.tile([P, (j1 - j0) * T], F32, name="x_raw_%d_%d" % (z, j0), align_bytes=256)
-            nc.sync.dma_start(out=x_raw[z, j0][:], in_=x_rows[z][:, j0 * T : j1 * T])
-            if (z, j0) == (0, 0):
-                nc.sync.dma_start(offsets[:], offs)
+        def load_x(z, j):
+            raw = sb.tile([P, T], F32, name="x_raw_%d_%d" % (z, j), align_bytes=256)
+            nc.sync.dma_start(out=raw[:], in_=x_rows[z][:, j * T : (j + 1) * T])
+            windows[z, j] = raw[:]
+
+        def load_w2(z):
+            for lo, hi, cut in W2_PIECES[z]:
+                name = "w2_raw_%d_%d" % (z, lo)
+                w2_raw[z, lo] = sb.tile([P, PACK, hi - lo], F32, name=name, tag=name, align_bytes=256)
+                nc.sync.dma_start(out=w2_raw[z, lo][:], in_=w2_rows[z][:, :, lo:hi])
+
         for z in range(PASSES):
-            w2_raw[z] = sb.tile([P, PACK, H], F32, name="w2_raw_%d" % z, align_bytes=256)
-            nc.sync.dma_start(out=w2_raw[z][:], in_=w2_rows[z])
+            for j in range(PACK):
+                load_x(z, j)
+                if (z, j) == (0, 0):
+                    nc.sync.dma_start(offsets[:], offs)
+        load_w2(0)
+        load_w2(1)
         nc.sync.dma_start(out=w1_codes[:].bitcast(I32), in_=w1_words.rearrange("z p c -> p z c").bitcast(I32))
         for q in range(4):
             nc.sync.dma_start(
@@ -68,67 +82,102 @@ def tile_picked_lora_none_e_kernel(
         def quantize(codes, sc, values):
             nc.vector.quantize_mx(out=codes.bitcast(FP8X4), scales=sc, in_=values)
 
-        x_codes = [sb.tile([P, S], U32, name="x_codes_%d" % z, align_bytes=64) for z in range(PASSES)]
-        x_sc = [sb.tile([P, S], U8, name="x_sc_%d" % z, align_bytes=64) for z in range(PASSES)]
+        x_bf, x_codes, x_sc = {}, {}, {}
 
         def group_cols(g):
             return slice(g * GROUP, (g + 1) * GROUP)
 
-        for z in range(PASSES):
-            planes = sb.tile([P, PACK, S], F32, name="planes_%d" % z, align_bytes=64)
-            for j0, j1 in [load[1:] for load in X_LOADS if load[0] == z]:
-                for j in range(j0, j1):
-                    window = x_raw[z, j0][:, (j - j0) * T : (j - j0 + 1) * T]
-                    nc.vector.tensor_copy(out=planes[:, j, :HALF_S], in_=window.indirect(offsets[:, : HALF_S // 16]))
-                    nc.scalar.activation(
-                        out=planes[:, j, HALF_S:], in_=window.indirect(offsets[:, HALF_S // 16 :]), func=COPY
-                    )
-            x_bf = [sb.tile([P, GROUP, PACK], BF16, name="x_bf_%d_%d" % (z, g), align_bytes=64) for g in range(GROUPS)]
-            for g in range(GROUPS):
-                copy = nc.vector.tensor_copy if g < GROUPS // 2 else nc.scalar.copy
-                copy(out=x_bf[g][:], in_=planes[:, :, group_cols(g)].rearrange("p j s -> p s j"))
-            for g in range(GROUPS):
-                quantize(x_codes[z][:, group_cols(g)], x_sc[z][:, group_cols(g)], x_bf[g][:].rearrange("p s j -> p (s j)"))
+        planes = [
+            sb.tile([P, PACK, S], F32, name="planes_%d" % z, tag="planes_%d" % z, align_bytes=256) for z in range(PASSES)
+        ]
+
+        def gather(z, j):
+            cut = HALF_S if (z, j) == (PASSES - 1, PACK - 1) else GATHER_CUT
+            window = windows[z, j]
+            nc.vector.tensor_copy(out=planes[z][:, j, :cut], in_=window.indirect(offsets[:, : cut // 16]))
+            nc.scalar.activation(out=planes[z][:, j, cut:], in_=window.indirect(offsets[:, cut // 16 :]), func=COPY)
+
+        def interleave(copy, z, g, tag):
+            x_bf[z, g] = sb.tile([P, GROUP, PACK], BF16, name="x_bf_%d_%d" % (z, g), tag=tag, align_bytes=256)
+            copy(
+                out=x_bf[z, g][:].rearrange("p (c i) j -> p c j i", i=4),
+                in_=planes[z][:, :, group_cols(g)].rearrange("p j (c i) -> p c j i", i=4),
+            )
+
+        def quantize_x(z, g, tag):
+            codes = sb.tile([P, GROUP], U32, name="x_codes_%d_%d" % (z, g), tag=tag, align_bytes=256)
+            sc = sb.tile([P, GROUP], U8, name="x_sc_%d_%d" % (z, g), align_bytes=64)
+            x_codes[z, g], x_sc[z, g] = codes[:], sc[:]
+            quantize(codes[:], sc[:], x_bf[z, g][:].rearrange("p s j -> p (s j)"))
 
         w2_codes = [sb.tile([P, PACK, P], U32, name="w2_codes_%d" % z, align_bytes=64) for z in range(PASSES)]
         w2_sc = [sb.tile([P, PACK, P], U8, name="w2_sc_%d" % z, align_bytes=64) for z in range(PASSES)]
         h_acc = [psum.tile([P, PACK, GROUP], F32, name="h_acc_%d" % g) for g in range(GROUPS)]
-        out_acc = [psum.tile([P, GROUP], F32, name="out_acc_%d" % g) for g in range(GROUPS)]
 
         def h_pass(z, g, t):
             nc.tensor.matmul_mx(
                 out=h_acc[g][:, t, :],
                 lhsT=w2_codes[z][:, t, :].bitcast(FP8X4),
                 lhsT_scale=w2_sc[z][:, t, :],
-                rhs=x_codes[z][:, group_cols(g)].bitcast(FP8X4),
-                rhs_scale=x_sc[z][:, group_cols(g)],
+                rhs=x_codes[z, g].bitcast(FP8X4),
+                rhs_scale=x_sc[z, g],
                 start=(z == 0 and t == 0),
                 stop=(z == PASSES - 1 and t == PACK - 1),
             )
 
-        for z in range(PASSES):
-            dealt = [sb.tile([P, 2, P, PACK], BF16, name="w2_dealt_%d_%d" % (z, v), align_bytes=64) for v in range(2)]
-            raw = w2_raw[z][:].rearrange("p j (m v e) -> p v m j e", v=2, e=2)
-            for copy, v, lo, hi in (
-                (nc.vector.tensor_copy, 0, 0, P),
-                (nc.scalar.copy, 1, 0, W2_CUT),
-                (nc.vector.tensor_copy, 1, W2_CUT, P),
-            ):
-                copy(out=dealt[v][:, :, lo:hi, :].rearrange("p e m j -> p m j e"), in_=raw[:, v, lo:hi])
-            for t in range(PACK):
-                quantize(w2_codes[z][:, t, :], w2_sc[z][:, t, :], dealt[t // 2][:, t % 2].rearrange("p m j -> p (m j)"))
-            for g0 in range(0, GROUPS, 2):
+        def quantize_w2(z):
+            dealt = [
+                sb.tile([P, PACK, HALF_P, PACK], BF16, name=name, tag=name, align_bytes=256)
+                for name in ("w2_dealt_%d_0" % z, "w2_dealt_%d_1" % z)
+            ]
+            for lo, hi, cut in W2_PIECES[z]:
+                half, m0 = divmod(lo // PACK, HALF_P)
+                dst = dealt[half][:, :, m0 : m0 + (hi - lo) // PACK, :].rearrange("p t m j -> p m j t")
+                raw = w2_raw[z, lo][:].rearrange("p j (m t) -> p m j t", t=PACK)
+                m = (cut - lo) // PACK
+                if cut > lo:
+                    nc.scalar.copy(out=dst[:, :m], in_=raw[:, :m])
+                if cut < hi:
+                    nc.vector.tensor_copy(out=dst[:, m:], in_=raw[:, m:])
+            for half in range(2):
+                cols = slice(half * HALF_P, (half + 1) * HALF_P)
                 for t in range(PACK):
-                    for g in (g0, g0 + 1):
-                        h_pass(z, g, t)
+                    quantize(w2_codes[z][:, t, cols], w2_sc[z][:, t, cols], dealt[half][:, t].rearrange("p m j -> p (m j)"))
+
+        for j in range(PACK):
+            gather(0, j)
+        for g in range(GROUPS):
+            interleave(nc.vector.tensor_copy, 0, g, "x_bf_0_%d" % g)
+        for g in range(GROUPS):
+            quantize_x(0, g, "x_codes_0_%d" % g)
+        for j in range(PACK):
+            gather(1, j)
+        interleave(nc.vector.tensor_copy, 1, 0, "x_bf_1_0")
+        interleave(nc.vector.tensor_copy, 1, 1, "x_bf_1_1")
+        quantize_w2(0)
+        for t in range(PACK):
+            for g in range(GROUPS):
+                h_pass(0, g, t)
+        interleave(nc.scalar.copy, 1, 2, "w2_raw_0_0")
+        interleave(nc.vector.tensor_copy, 1, 3, "w2_raw_0_256")
+        for g in range(2):
+            quantize_x(1, g, "x_codes_1_%d" % g)
+        quantize_w2(1)
+        quantize_x(1, 2, "x_codes_1_2")
+        quantize_x(1, 3, "w2_dealt_1_1")
+        for g in range(GROUPS):
+            for t in range(PACK):
+                h_pass(1, g, t)
+
+        out_acc = [psum.tile([P, GROUP], F32, name="out_acc_%d" % g) for g in range(GROUPS)]
         for g in range(GROUPS):
             for z in range(PASSES):
                 nc.tensor.matmul_mx(
                     out=out_acc[g][:],
                     lhsT=w1_codes[:, z, :].bitcast(FP4X4),
                     lhsT_scale=w1_sc[:, z, :],
-                    rhs=x_codes[z][:, group_cols(g)].bitcast(FP8X4),
-                    rhs_scale=x_sc[z][:, group_cols(g)],
+                    rhs=x_codes[z, g].bitcast(FP8X4),
+                    rhs_scale=x_sc[z, g],
                     start=(z == 0),
                     stop=False,
                 )

@@ -21,11 +21,11 @@ PASSES = K // (P * PACK)
 GROUP = 128
 GROUPS = S // GROUP
 HALF_S = S // 2
-HALF_P = P // 2
+PUT_OFF = 2
 GATHER_CUT = 192
 W2_PIECES = [
     [(0, 256, 256), (256, 512, 336)],
-    [(0, 256, 168), (256, 384, 336), (384, 512, 448)],
+    [(0, 256, 96), (256, 384, 352), (384, 512, None)],
 ]
 
 
@@ -91,83 +91,97 @@ def tile_picked_lora_none_e_kernel(
             sb.tile([P, PACK, S], F32, name="planes_%d" % z, tag="planes_%d" % z, align_bytes=256) for z in range(PASSES)
         ]
 
-        def gather(z, j):
-            cut = HALF_S if (z, j) == (PASSES - 1, PACK - 1) else GATHER_CUT
+        def gather(z, j, cuts):
             window = windows[z, j]
-            nc.vector.tensor_copy(out=planes[z][:, j, :cut], in_=window.indirect(offsets[:, : cut // 16]))
-            nc.scalar.activation(out=planes[z][:, j, cut:], in_=window.indirect(offsets[:, cut // 16 :]), func=COPY)
+            nc.vector.tensor_copy(out=planes[z][:, j, : cuts[0]], in_=window.indirect(offsets[:, : cuts[0] // 16]))
+            for lo, hi in zip(cuts, cuts[1:] + [S]):
+                nc.scalar.activation(
+                    out=planes[z][:, j, lo:hi], in_=window.indirect(offsets[:, lo // 16 : hi // 16]), func=COPY
+                )
 
-        def interleave(copy, z, g, tag):
+        def interleave(z, g, tag, cut):
             x_bf[z, g] = sb.tile([P, GROUP, PACK], BF16, name="x_bf_%d_%d" % (z, g), tag=tag, align_bytes=256)
-            copy(
-                out=x_bf[z, g][:].rearrange("p (c i) j -> p c j i", i=4),
-                in_=planes[z][:, :, group_cols(g)].rearrange("p j (c i) -> p c j i", i=4),
-            )
+            dst = x_bf[z, g][:].rearrange("p (c i) j -> p c j i", i=4)
+            src = planes[z][:, :, group_cols(g)].rearrange("p j (c i) -> p c j i", i=4)
+            if cut > 0:
+                nc.scalar.copy(out=dst[:, : cut // 4], in_=src[:, : cut // 4])
+            if cut < GROUP:
+                nc.vector.tensor_copy(out=dst[:, cut // 4 :], in_=src[:, cut // 4 :])
 
-        def quantize_x(z, g, tag):
-            codes = sb.tile([P, GROUP], U32, name="x_codes_%d_%d" % (z, g), tag=tag, align_bytes=256)
-            sc = sb.tile([P, GROUP], U8, name="x_sc_%d_%d" % (z, g), align_bytes=64)
-            x_codes[z, g], x_sc[z, g] = codes[:], sc[:]
-            quantize(codes[:], sc[:], x_bf[z, g][:].rearrange("p s j -> p (s j)"))
+        def quantize_x(z, groups, tag):
+            width = len(groups) * GROUP
+            codes = sb.tile([P, width], U32, name="x_codes_%d_%d" % (z, groups[0]), tag=tag, align_bytes=256)
+            sc = sb.tile([P, width], U8, name="x_sc_%d_%d" % (z, groups[0]), align_bytes=64)
+            for e, g in enumerate(groups):
+                x_codes[z, g], x_sc[z, g] = codes[:, group_cols(e)], sc[:, group_cols(e)]
+                quantize(x_codes[z, g], x_sc[z, g], x_bf[z, g][:].rearrange("p s j -> p (s j)"))
 
         w2_codes = [sb.tile([P, PACK, P], U32, name="w2_codes_%d" % z, align_bytes=64) for z in range(PASSES)]
         w2_sc = [sb.tile([P, PACK, P], U8, name="w2_sc_%d" % z, align_bytes=64) for z in range(PASSES)]
         h_acc = [psum.tile([P, PACK, GROUP], F32, name="h_acc_%d" % g) for g in range(GROUPS)]
 
-        def h_pass(z, g, t):
+        def h_pass(z, g, t, start=False, stop=False):
             nc.tensor.matmul_mx(
                 out=h_acc[g][:, t, :],
                 lhsT=w2_codes[z][:, t, :].bitcast(FP8X4),
                 lhsT_scale=w2_sc[z][:, t, :],
                 rhs=x_codes[z, g].bitcast(FP8X4),
                 rhs_scale=x_sc[z, g],
-                start=(z == 0 and t == 0),
-                stop=(z == PASSES - 1 and t == PACK - 1),
+                start=start,
+                stop=stop,
             )
 
         def quantize_w2(z):
-            dealt = [
-                sb.tile([P, PACK, HALF_P, PACK], BF16, name=name, tag=name, align_bytes=256)
-                for name in ("w2_dealt_%d_0" % z, "w2_dealt_%d_1" % z)
-            ]
+            dealt = {}
             for lo, hi, cut in W2_PIECES[z]:
-                half, m0 = divmod(lo // PACK, HALF_P)
-                dst = dealt[half][:, :, m0 : m0 + (hi - lo) // PACK, :].rearrange("p t m j -> p m j t")
+                name = "w2_dealt_%d_%d" % (z, lo)
+                dealt[lo, hi] = sb.tile([P, PACK, (hi - lo) // PACK, PACK], BF16, name=name, tag=name, align_bytes=256)
+                dst = dealt[lo, hi][:].rearrange("p t m j -> p m j t")
                 raw = w2_raw[z, lo][:].rearrange("p j (m t) -> p m j t", t=PACK)
+                if cut is None:
+                    nc.scalar.copy(out=dst[:, :, :, :2], in_=raw[:, :, :, :2])
+                    nc.vector.tensor_copy(out=dst[:, :, :, 2:], in_=raw[:, :, :, 2:])
+                    continue
                 m = (cut - lo) // PACK
                 if cut > lo:
                     nc.scalar.copy(out=dst[:, :m], in_=raw[:, :m])
                 if cut < hi:
                     nc.vector.tensor_copy(out=dst[:, m:], in_=raw[:, m:])
-            for half in range(2):
-                cols = slice(half * HALF_P, (half + 1) * HALF_P)
-                for t in range(PACK):
-                    quantize(w2_codes[z][:, t, cols], w2_sc[z][:, t, cols], dealt[half][:, t].rearrange("p m j -> p (m j)"))
+            if z == 0:
+                calls = [(piece, t) for t in range(PACK) for piece in dealt]
+            else:
+                calls = [(piece, t) for piece in dealt for t in range(PACK)]
+            for (lo, hi), t in calls:
+                cols = slice(lo // PACK, hi // PACK)
+                quantize(w2_codes[z][:, t, cols], w2_sc[z][:, t, cols], dealt[lo, hi][:, t].rearrange("p m j -> p (m j)"))
 
         for j in range(PACK):
-            gather(0, j)
+            gather(0, j, [GATHER_CUT])
         for g in range(GROUPS):
-            interleave(nc.vector.tensor_copy, 0, g, "x_bf_0_%d" % g)
-        for g in range(GROUPS):
-            quantize_x(0, g, "x_codes_0_%d" % g)
-        for j in range(PACK):
-            gather(1, j)
-        interleave(nc.vector.tensor_copy, 1, 0, "x_bf_1_0")
-        interleave(nc.vector.tensor_copy, 1, 1, "x_bf_1_1")
+            interleave(0, g, "x_bf_0_%d" % g, 0)
+        quantize_x(0, [0, 1, 2, 3], "x_codes_0")
+        for j in range(PACK - 1):
+            gather(1, j, [GATHER_CUT])
+        gather(1, PACK - 1, [GROUP, 2 * GROUP])
+        for g in (1, 0, 2):
+            interleave(1, g, "x_bf_1_%d" % g, 0)
         quantize_w2(0)
+        put_off = [(GROUPS - 1, t) for t in range(PACK - PUT_OFF, PACK)]
         for t in range(PACK):
             for g in range(GROUPS):
-                h_pass(0, g, t)
-        interleave(nc.scalar.copy, 1, 2, "w2_raw_0_0")
-        interleave(nc.vector.tensor_copy, 1, 3, "w2_raw_0_256")
-        for g in range(2):
-            quantize_x(1, g, "x_codes_1_%d" % g)
+                if (g, t) not in put_off:
+                    h_pass(0, g, t, start=(t == 0))
+        interleave(1, 3, "w2_raw_0_0", GROUP)
+        quantize_x(1, [0, 1, 2], "x_codes_1")
         quantize_w2(1)
-        quantize_x(1, 2, "x_codes_1_2")
-        quantize_x(1, 3, "w2_dealt_1_1")
+        quantize_x(1, [3], "w2_dealt_1_384")
         for g in range(GROUPS):
+            h_pass(1, g, 0)
             for t in range(PACK):
-                h_pass(1, g, t)
+                if (g, t) in put_off:
+                    h_pass(0, g, t)
+            for t in range(1, PACK):
+                h_pass(1, g, t, stop=(t == PACK - 1))
 
         out_acc = [psum.tile([P, GROUP], F32, name="out_acc_%d" % g) for g in range(GROUPS)]
         for g in range(GROUPS):

@@ -82,7 +82,7 @@ def tile_picked_lora_none_e_kernel(
         def quantize(codes, sc, values):
             nc.vector.quantize_mx(out=codes.bitcast(FP8X4), scales=sc, in_=values)
 
-        x_bf, x_codes, x_sc = {}, {}, {}
+        x_bf, x_codes, x_sc, x_tiles = {}, {}, {}, {}
 
         def group_cols(g):
             return slice(g * GROUP, (g + 1) * GROUP)
@@ -112,6 +112,7 @@ def tile_picked_lora_none_e_kernel(
             width = len(groups) * GROUP
             codes = sb.tile([P, width], U32, name="x_codes_%d_%d" % (z, groups[0]), tag=tag, align_bytes=256)
             sc = sb.tile([P, width], U8, name="x_sc_%d_%d" % (z, groups[0]), align_bytes=64)
+            x_tiles[z, groups[0]] = codes, sc
             for e, g in enumerate(groups):
                 x_codes[z, g], x_sc[z, g] = codes[:, group_cols(e)], sc[:, group_cols(e)]
                 quantize(x_codes[z, g], x_sc[z, g], x_bf[z, g][:].rearrange("p s j -> p (s j)"))
@@ -166,13 +167,23 @@ def tile_picked_lora_none_e_kernel(
         for g in (1, 0, 2):
             interleave(1, g, "x_bf_1_%d" % g, 0)
         quantize_w2(0)
+        quantize_x(1, [0, 1, 2], "x_codes_1")
+        warm = psum.tile([P, S], F32, name="warm", tag="out_acc_3")
+        nc.tensor.matmul_mx(
+            out=warm[:],
+            lhsT=x_codes[1, 2].bitcast(FP8X4),
+            lhsT_scale=x_sc[1, 2],
+            rhs=x_tiles[0, 0][0][:].bitcast(FP8X4),
+            rhs_scale=x_tiles[0, 0][1][:],
+            start=True,
+            stop=True,
+        )
         put_off = [(GROUPS - 1, t) for t in range(PACK - PUT_OFF, PACK)]
         for t in range(PACK):
             for g in range(GROUPS):
                 if (g, t) not in put_off:
                     h_pass(0, g, t, start=(t == 0))
         interleave(1, 3, "w2_raw_0_0", GROUP)
-        quantize_x(1, [0, 1, 2], "x_codes_1")
         quantize_w2(1)
         quantize_x(1, [3], "w2_dealt_1_384")
         for g in range(GROUPS):
@@ -183,7 +194,7 @@ def tile_picked_lora_none_e_kernel(
             for t in range(1, PACK):
                 h_pass(1, g, t, stop=(t == PACK - 1))
 
-        out_acc = [psum.tile([P, GROUP], F32, name="out_acc_%d" % g) for g in range(GROUPS)]
+        out_acc = [psum.tile([P, GROUP], F32, name="out_acc_%d" % g, tag="out_acc_%d" % g) for g in range(GROUPS)]
         for g in range(GROUPS):
             for z in range(PASSES):
                 nc.tensor.matmul_mx(

@@ -21,12 +21,11 @@ PASSES = K // (P * PACK)
 GROUP = 128
 GROUPS = S // GROUP
 HALF_S = S // 2
-PUT_OFF = 2
+PUT_OFF = 1
 GATHER_CUT = 192
-W2_PIECES = [
-    [(0, 256, 256), (256, 512, 336)],
-    [(0, 256, 96), (256, 384, 352), (384, 512, None)],
-]
+PAIR_CUT = 64
+LAST_CUTS = [112, 352]
+W2_PIECES = [[(0, 256), (256, 512)], [(0, 256), (256, 384), (384, 512)]]
 
 
 def tile_picked_lora_none_e_kernel(
@@ -55,7 +54,7 @@ def tile_picked_lora_none_e_kernel(
             windows[z, j] = raw[:]
 
         def load_w2(z):
-            for lo, hi, cut in W2_PIECES[z]:
+            for lo, hi in W2_PIECES[z]:
                 name = "w2_raw_%d_%d" % (z, lo)
                 w2_raw[z, lo] = sb.tile([P, PACK, hi - lo], F32, name=name, tag=name, align_bytes=256)
                 nc.sync.dma_start(out=w2_raw[z, lo][:], in_=w2_rows[z][:, :, lo:hi])
@@ -117,44 +116,42 @@ def tile_picked_lora_none_e_kernel(
                 x_codes[z, g], x_sc[z, g] = codes[:, group_cols(e)], sc[:, group_cols(e)]
                 quantize(x_codes[z, g], x_sc[z, g], x_bf[z, g][:].rearrange("p s j -> p (s j)"))
 
-        w2_codes = [sb.tile([P, PACK, P], U32, name="w2_codes_%d" % z, align_bytes=64) for z in range(PASSES)]
-        w2_sc = [sb.tile([P, PACK, P], U8, name="w2_sc_%d" % z, align_bytes=64) for z in range(PASSES)]
+        w2_codes, w2_sc = {}, {}
         h_acc = [psum.tile([P, PACK, GROUP], F32, name="h_acc_%d" % g) for g in range(GROUPS)]
 
         def h_pass(z, g, t, start=False, stop=False):
             nc.tensor.matmul_mx(
                 out=h_acc[g][:, t, :],
-                lhsT=w2_codes[z][:, t, :].bitcast(FP8X4),
-                lhsT_scale=w2_sc[z][:, t, :],
+                lhsT=w2_codes[z, t].bitcast(FP8X4),
+                lhsT_scale=w2_sc[z, t],
                 rhs=x_codes[z, g].bitcast(FP8X4),
                 rhs_scale=x_sc[z, g],
                 start=start,
                 stop=stop,
             )
 
-        def quantize_w2(z):
-            dealt = {}
-            for lo, hi, cut in W2_PIECES[z]:
-                name = "w2_dealt_%d_%d" % (z, lo)
-                dealt[lo, hi] = sb.tile([P, PACK, (hi - lo) // PACK, PACK], BF16, name=name, tag=name, align_bytes=256)
-                dst = dealt[lo, hi][:].rearrange("p t m j -> p m j t")
-                raw = w2_raw[z, lo][:].rearrange("p j (m t) -> p m j t", t=PACK)
-                if cut is None:
-                    nc.scalar.copy(out=dst[:, :, :, :2], in_=raw[:, :, :, :2])
-                    nc.vector.tensor_copy(out=dst[:, :, :, 2:], in_=raw[:, :, :, 2:])
-                    continue
-                m = (cut - lo) // PACK
-                if cut > lo:
-                    nc.scalar.copy(out=dst[:, :m], in_=raw[:, :m])
-                if cut < hi:
-                    nc.vector.tensor_copy(out=dst[:, m:], in_=raw[:, m:])
-            if z == 0:
-                calls = [(piece, t) for t in range(PACK) for piece in dealt]
-            else:
-                calls = [(piece, t) for piece in dealt for t in range(PACK)]
-            for (lo, hi), t in calls:
-                cols = slice(lo // PACK, hi // PACK)
-                quantize(w2_codes[z][:, t, cols], w2_sc[z][:, t, cols], dealt[lo, hi][:, t].rearrange("p m j -> p (m j)"))
+        def stationary_tiles(z, t0, t1, tag):
+            codes = sb.tile([P, t1 - t0, P], U32, name="w2_codes_%d_%d" % (z, t0), tag=tag, align_bytes=256)
+            sc = sb.tile([P, t1 - t0, P], U8, name="w2_sc_%d_%d" % (z, t0), align_bytes=64)
+            for t in range(t0, t1):
+                w2_codes[z, t], w2_sc[z, t] = codes[:, t - t0, :], sc[:, t - t0, :]
+
+        def deal(z, lo, hi, t0, t1, cut):
+            name = "w2_dealt_%d_%d_%d" % (z, lo, t0)
+            dealt = sb.tile([P, t1 - t0, (hi - lo) // PACK, PACK], BF16, name=name, tag=name, align_bytes=256)
+            dst = dealt[:].rearrange("p t m j -> p m j t")
+            raw = w2_raw[z, lo][:].rearrange("p j (m t) -> p m j t", t=PACK)[:, :, :, t0:t1]
+            m = (cut - lo) // PACK
+            if cut < hi:
+                nc.vector.tensor_copy(out=dst[:, m:], in_=raw[:, m:])
+            if cut > lo:
+                nc.scalar.copy(out=dst[:, :m], in_=raw[:, :m])
+            return {t: dealt[:, t - t0] for t in range(t0, t1)}
+
+        def quantize_w2(z, lo, hi, dealt, tiles):
+            cols = slice(lo // PACK, hi // PACK)
+            for t in tiles:
+                quantize(w2_codes[z, t][:, cols], w2_sc[z, t][:, cols], dealt[t].rearrange("p m j -> p (m j)"))
 
         for j in range(PACK):
             gather(0, j, [GATHER_CUT])
@@ -164,15 +161,23 @@ def tile_picked_lora_none_e_kernel(
         for j in range(PACK - 1):
             gather(1, j, [GATHER_CUT])
         gather(1, PACK - 1, [GROUP, 2 * GROUP])
-        for g in (1, 0, 2):
+        for g in (1, 0, 2, 3):
             interleave(1, g, "x_bf_1_%d" % g, 0)
-        quantize_w2(0)
-        quantize_x(1, [0, 1, 2], "x_codes_1")
+        first = deal(0, 0, 256, 0, 4, 256)
+        second_lo = deal(0, 256, 512, 0, 2, 256 + PAIR_CUT)
+        second_hi = deal(0, 256, 512, 2, 4, 512 - PAIR_CUT)
+        stationary_tiles(0, 0, 2, "w2_codes_0")
+        quantize_w2(0, 0, 256, first, (0, 1))
+        quantize_w2(0, 256, 512, second_lo, (0, 1))
+        stationary_tiles(0, 2, 4, "w2_dealt_0_256_0")
+        quantize_w2(0, 0, 256, first, (2, 3))
+        quantize_w2(0, 256, 512, second_hi, (2, 3))
+        quantize_x(1, [0, 1], "x_codes_1")
         warm = psum.tile([P, S], F32, name="warm", tag="out_acc_3")
         nc.tensor.matmul_mx(
             out=warm[:],
-            lhsT=x_codes[1, 2].bitcast(FP8X4),
-            lhsT_scale=x_sc[1, 2],
+            lhsT=x_codes[1, 0].bitcast(FP8X4),
+            lhsT_scale=x_sc[1, 0],
             rhs=x_tiles[0, 0][0][:].bitcast(FP8X4),
             rhs_scale=x_tiles[0, 0][1][:],
             start=True,
@@ -183,9 +188,12 @@ def tile_picked_lora_none_e_kernel(
             for g in range(GROUPS):
                 if (g, t) not in put_off:
                     h_pass(0, g, t, start=(t == 0))
-        interleave(1, 3, "w2_raw_0_0", GROUP)
-        quantize_w2(1)
-        quantize_x(1, [3], "w2_dealt_1_384")
+        stationary_tiles(1, 0, 4, "w2_codes_1")
+        pieces = [deal(1, 0, 256, 0, 4, LAST_CUTS[0]), deal(1, 256, 384, 0, 4, LAST_CUTS[1])]
+        pieces.append({**deal(1, 384, 512, 0, 2, 384), **deal(1, 384, 512, 2, 4, 512)})
+        for (lo, hi), dealt in zip(W2_PIECES[1], pieces):
+            quantize_w2(1, lo, hi, dealt, range(PACK))
+        quantize_x(1, [2, 3], "w2_dealt_1_384_0")
         for g in range(GROUPS):
             h_pass(1, g, 0)
             for t in range(PACK):

@@ -23,6 +23,8 @@ GROUPS = S // GROUP
 HALF_S = S // 2
 PUT_OFF = 1
 GATHER_CUT = 192
+FIRST_CUT = 256
+X_LOADS = [[(0, 2), (2, 3), (3, 4)], [(0, 1), (1, 2), (2, 3), (3, 4)]]
 PAIR_CUT = 64
 LAST_CUTS = [112, 352]
 W2_PIECES = [[(0, 256), (256, 512)], [(0, 256), (256, 384), (384, 512)]]
@@ -48,10 +50,11 @@ def tile_picked_lora_none_e_kernel(
         w2_rows = w2.rearrange("(z p j) i -> z p j i", z=PASSES, p=P, j=PACK)
         windows, w2_raw = {}, {}
 
-        def load_x(z, j):
-            raw = sb.tile([P, T], F32, name="x_raw_%d_%d" % (z, j), align_bytes=256)
-            nc.sync.dma_start(out=raw[:], in_=x_rows[z][:, j * T : (j + 1) * T])
-            windows[z, j] = raw[:]
+        def load_x(z, j0, j1):
+            raw = sb.tile([P, (j1 - j0) * T], F32, name="x_raw_%d_%d" % (z, j0), align_bytes=256)
+            nc.sync.dma_start(out=raw[:], in_=x_rows[z][:, j0 * T : j1 * T])
+            for j in range(j0, j1):
+                windows[z, j] = raw[:, (j - j0) * T : (j - j0 + 1) * T]
 
         def load_w2(z):
             for lo, hi in W2_PIECES[z]:
@@ -60,13 +63,14 @@ def tile_picked_lora_none_e_kernel(
                 nc.sync.dma_start(out=w2_raw[z, lo][:], in_=w2_rows[z][:, :, lo:hi])
 
         for z in range(PASSES):
-            for j in range(PACK):
-                load_x(z, j)
-                if (z, j) == (0, 0):
+            for j0, j1 in X_LOADS[z]:
+                load_x(z, j0, j1)
+                if (z, j0) == (0, 0):
                     nc.sync.dma_start(offsets[:], offs)
         load_w2(0)
         load_w2(1)
-        nc.sync.dma_start(out=w1_codes[:].bitcast(I32), in_=w1_words.rearrange("z p c -> p z c").bitcast(I32))
+        for z in range(PASSES):
+            nc.sync.dma_start(out=w1_codes[:, z, :].bitcast(I32), in_=w1_words[z].bitcast(I32))
         for q in range(4):
             nc.sync.dma_start(
                 out=w1_sc[32 * q : 32 * q + 4, :, :].bitcast(I32),
@@ -154,7 +158,7 @@ def tile_picked_lora_none_e_kernel(
                 quantize(w2_codes[z, t][:, cols], w2_sc[z, t][:, cols], dealt[t].rearrange("p m j -> p (m j)"))
 
         for j in range(PACK):
-            gather(0, j, [GATHER_CUT])
+            gather(0, j, [FIRST_CUT])
         for g in range(GROUPS):
             interleave(0, g, "x_bf_0_%d" % g, 0)
         quantize_x(0, [0, 1, 2, 3], "x_codes_0")

@@ -22,9 +22,8 @@ GROUP = 128
 GROUPS = S // GROUP
 HALF_S = S // 2
 PUT_OFF = 1
-GATHER_CUT = 192
-FIRST_CUT = 256
-X_LOADS = [[(0, 2), (2, 3), (3, 4)], [(0, 1), (1, 2), (2, 3), (3, 4)]]
+GATHER_CUTS = [[288, 256, 256, 320], [288, 256, 256]]
+X_LOADS = [[(0, 2), (2, 3), (3, 4)], [(0, 2), (2, 3), (3, 4)]]
 PAIR_CUT = 64
 LAST_CUTS = [112, 352]
 W2_PIECES = [[(0, 256), (256, 512)], [(0, 256), (256, 384), (384, 512)]]
@@ -69,8 +68,7 @@ def tile_picked_lora_none_e_kernel(
                     nc.sync.dma_start(offsets[:], offs)
         load_w2(0)
         load_w2(1)
-        for z in range(PASSES):
-            nc.sync.dma_start(out=w1_codes[:, z, :].bitcast(I32), in_=w1_words[z].bitcast(I32))
+        nc.sync.dma_start(out=w1_codes[:].bitcast(I32), in_=w1_words.rearrange("z p c -> p z c").bitcast(I32))
         for q in range(4):
             nc.sync.dma_start(
                 out=w1_sc[32 * q : 32 * q + 4, :, :].bitcast(I32),
@@ -78,7 +76,8 @@ def tile_picked_lora_none_e_kernel(
             )
         nc.sync.dma_start(out=w3_codes[:].bitcast(I32), in_=w3_words[0].bitcast(I32))
         for q in range(4):
-            nc.sync.dma_start(
+            queue = nc.gpsimd if q < 2 else nc.sync
+            queue.dma_start(
                 out=w3_sc[32 * q : 32 * q + 4, :].bitcast(I32), in_=w3_scales[0, 4 * q : 4 * q + 4, :].bitcast(I32)
             )
 
@@ -94,9 +93,11 @@ def tile_picked_lora_none_e_kernel(
             sb.tile([P, PACK, S], F32, name="planes_%d" % z, tag="planes_%d" % z, align_bytes=256) for z in range(PASSES)
         ]
 
-        def gather(z, j, cuts):
+        def gather(z, j, cuts, first=()):
             window = windows[z, j]
-            nc.vector.tensor_copy(out=planes[z][:, j, : cuts[0]], in_=window.indirect(offsets[:, : cuts[0] // 16]))
+            edges = [0, *first, cuts[0]]
+            for lo, hi in zip(edges, edges[1:]):
+                nc.vector.tensor_copy(out=planes[z][:, j, lo:hi], in_=window.indirect(offsets[:, lo // 16 : hi // 16]))
             for lo, hi in zip(cuts, cuts[1:] + [S]):
                 nc.scalar.activation(
                     out=planes[z][:, j, lo:hi], in_=window.indirect(offsets[:, lo // 16 : hi // 16]), func=COPY
@@ -111,13 +112,14 @@ def tile_picked_lora_none_e_kernel(
             if cut < GROUP:
                 nc.vector.tensor_copy(out=dst[:, cut // 4 :], in_=src[:, cut // 4 :])
 
-        def quantize_x(z, groups, tag):
+        def quantize_x(z, groups, tag, order=None):
             width = len(groups) * GROUP
             codes = sb.tile([P, width], U32, name="x_codes_%d_%d" % (z, groups[0]), tag=tag, align_bytes=256)
             sc = sb.tile([P, width], U8, name="x_sc_%d_%d" % (z, groups[0]), align_bytes=64)
             x_tiles[z, groups[0]] = codes, sc
             for e, g in enumerate(groups):
                 x_codes[z, g], x_sc[z, g] = codes[:, group_cols(e)], sc[:, group_cols(e)]
+            for g in order or groups:
                 quantize(x_codes[z, g], x_sc[z, g], x_bf[z, g][:].rearrange("p s j -> p (s j)"))
 
         w2_codes, w2_sc = {}, {}
@@ -158,12 +160,12 @@ def tile_picked_lora_none_e_kernel(
                 quantize(w2_codes[z, t][:, cols], w2_sc[z, t][:, cols], dealt[t].rearrange("p m j -> p (m j)"))
 
         for j in range(PACK):
-            gather(0, j, [FIRST_CUT])
-        for g in range(GROUPS):
-            interleave(0, g, "x_bf_0_%d" % g, 0)
-        quantize_x(0, [0, 1, 2, 3], "x_codes_0")
+            gather(0, j, [GATHER_CUTS[0][j]], first=(GROUP,) if j == PACK - 1 else ())
+        for g in (3, 0, 2, 1):
+            interleave(0, g, "x_bf_0_%d" % g, GROUP if g < 2 else 0)
+        quantize_x(0, [0, 1, 2, 3], "x_codes_0", order=(3, 0, 2, 1))
         for j in range(PACK - 1):
-            gather(1, j, [GATHER_CUT])
+            gather(1, j, [GATHER_CUTS[1][j]])
         gather(1, PACK - 1, [GROUP, 2 * GROUP])
         for g in (1, 0, 2, 3):
             interleave(1, g, "x_bf_1_%d" % g, 0)

@@ -21,9 +21,10 @@ PASSES = K // (P * PACK)
 GROUP = 128
 GROUPS = S // GROUP
 HALF_S = S // 2
-PUT_OFF = 1
+PUT_OFF = 0
 GATHER_CUTS = [[288, 256, 256, 320], [288, 256, 256]]
 X_LOADS = [[(0, 2), (2, 3), (3, 4)], [(0, 2), (2, 3), (3, 4)]]
+STORE_OF = [(0, 1), (0, 1), (2, 2), (3, 3)]
 PAIR_CUT = 64
 LAST_CUTS = [112, 352]
 W2_PIECES = [[(0, 256), (256, 512)], [(0, 256), (256, 384), (384, 512)]]
@@ -68,7 +69,8 @@ def tile_picked_lora_none_e_kernel(
                     nc.sync.dma_start(offsets[:], offs)
         load_w2(0)
         load_w2(1)
-        nc.sync.dma_start(out=w1_codes[:].bitcast(I32), in_=w1_words.rearrange("z p c -> p z c").bitcast(I32))
+        for z in range(PASSES):
+            nc.sync.dma_start(out=w1_codes[:, z, :].bitcast(I32), in_=w1_words[z].bitcast(I32))
         for q in range(4):
             nc.sync.dma_start(
                 out=w1_sc[32 * q : 32 * q + 4, :, :].bitcast(I32),
@@ -239,7 +241,10 @@ def tile_picked_lora_none_e_kernel(
                 start=False,
                 stop=True,
             )
-            res = sb.tile([P, GROUP], F32, name="res_%d" % g, align_bytes=256)
+            first, last = STORE_OF[g]
+            if g == first:
+                res = sb.tile([P, (last - first + 1) * GROUP], F32, name="res_%d" % g, align_bytes=256)
             copy = nc.vector.tensor_copy if g == GROUPS - 1 else nc.scalar.copy
-            copy(out=res[:], in_=out_acc[g][:])
-            nc.sync.dma_start(out=out[:, group_cols(g)], in_=res[:])
+            copy(out=res[:, group_cols(g - first)], in_=out_acc[g][:])
+            if g == last:
+                nc.sync.dma_start(out=out[:, first * GROUP : (last + 1) * GROUP], in_=res[:])

@@ -24,7 +24,7 @@ HALF_S = S // 2
 PUT_OFF = 0
 GATHER_CUTS = [[288, 256, 256, 320], [288, 256, 256]]
 X_LOADS = [[(0, 2), (2, 3), (3, 4)], [(0, 2), (2, 3), (3, 4)]]
-STORE_OF = [(0, 1), (0, 1), (2, 2), (3, 3)]
+STORE_OF = [(0, 1), (0, 1), (2, 3), (2, 3)]
 PAIR_CUT = 64
 LAST_CUTS = [112, 352]
 W2_PIECES = [[(0, 256), (256, 512)], [(0, 256), (256, 384), (384, 512)]]
@@ -69,8 +69,7 @@ def tile_picked_lora_none_e_kernel(
                     nc.sync.dma_start(offsets[:], offs)
         load_w2(0)
         load_w2(1)
-        for z in range(PASSES):
-            nc.sync.dma_start(out=w1_codes[:, z, :].bitcast(I32), in_=w1_words[z].bitcast(I32))
+        nc.sync.dma_start(out=w1_codes[:].bitcast(I32), in_=w1_words.rearrange("z p c -> p z c").bitcast(I32))
         for q in range(4):
             nc.sync.dma_start(
                 out=w1_sc[32 * q : 32 * q + 4, :, :].bitcast(I32),
@@ -78,8 +77,7 @@ def tile_picked_lora_none_e_kernel(
             )
         nc.sync.dma_start(out=w3_codes[:].bitcast(I32), in_=w3_words[0].bitcast(I32))
         for q in range(4):
-            queue = nc.gpsimd if q < 2 else nc.sync
-            queue.dma_start(
+            nc.sync.dma_start(
                 out=w3_sc[32 * q : 32 * q + 4, :].bitcast(I32), in_=w3_scales[0, 4 * q : 4 * q + 4, :].bitcast(I32)
             )
 
@@ -244,7 +242,7 @@ def tile_picked_lora_none_e_kernel(
             first, last = STORE_OF[g]
             if g == first:
                 res = sb.tile([P, (last - first + 1) * GROUP], F32, name="res_%d" % g, align_bytes=256)
-            copy = nc.vector.tensor_copy if g == GROUPS - 1 else nc.scalar.copy
+            copy = nc.vector.tensor_copy if g == GROUPS - 2 else nc.scalar.copy
             copy(out=res[:, group_cols(g - first)], in_=out_acc[g][:])
             if g == last:
                 nc.sync.dma_start(out=out[:, first * GROUP : (last + 1) * GROUP], in_=res[:])

@@ -25,6 +25,7 @@ PUT_OFF = 0
 GATHER_CUTS = [[288, 256, 256, 320], [288, 256, 256]]
 X_LOADS = [[(0, 2), (2, 3), (3, 4)], [(0, 2), (2, 3), (3, 4)]]
 STORE_OF = [(0, 1), (0, 1), (2, 3), (2, 3)]
+CODE_SHIFT = 32
 PAIR_CUT = 64
 LAST_CUTS = [112, 352]
 W2_PIECES = [[(0, 256), (256, 512)], [(0, 256), (256, 384), (384, 512)]]
@@ -137,10 +138,12 @@ def tile_picked_lora_none_e_kernel(
             )
 
         def stationary_tiles(z, t0, t1, tag):
-            codes = sb.tile([P, t1 - t0, P], U32, name="w2_codes_%d_%d" % (z, t0), tag=tag, align_bytes=256)
+            width = (t1 - t0) * P + 2 * CODE_SHIFT
+            codes = sb.tile([P, width], U32, name="w2_codes_%d_%d" % (z, t0), tag=tag, align_bytes=256)
             sc = sb.tile([P, t1 - t0, P], U8, name="w2_sc_%d_%d" % (z, t0), align_bytes=64)
             for t in range(t0, t1):
-                w2_codes[z, t], w2_sc[z, t] = codes[:, t - t0, :], sc[:, t - t0, :]
+                start = CODE_SHIFT + (t - t0) * P
+                w2_codes[z, t], w2_sc[z, t] = codes[:, start : start + P], sc[:, t - t0, :]
 
         def deal(z, lo, hi, t0, t1, cut):
             name = "w2_dealt_%d_%d_%d" % (z, lo, t0)

from contextlib import ExitStack

import concourse.mybir as mybir

K, T, S, H, N = 1024, 1024, 512, 512, 128
FLOPS = 2 * S * (K * H + K * N + H * N)

F32 = mybir.dt.float32
BF16 = mybir.dt.bfloat16
I32 = mybir.dt.int32
U32 = mybir.dt.uint32
U16 = mybir.dt.uint16
U8 = mybir.dt.uint8
FP8X4 = mybir.dt.float8_e4m3fn_x4
FP4X4 = mybir.dt.float4_e2m1fn_x4
COPY = mybir.ActivationFunctionType.Copy

P = 128
PACK = 4
PASSES = K // (P * PACK)
GROUP = 128
GROUPS = S // GROUP
HALF_S = S // 2
PUT_OFF = 0
GATHER_CUTS = [[288, 256, 256, 320], [288, 256, 256]]
X_LOADS = [[(0, 2), (2, 3), (3, 4)], [(0, 2), (2, 3), (3, 4)]]
STORE_OF = [(0, 1), (0, 1), (2, 3), (2, 3)]
CODE_SHIFT = 32
PAIR_CUT = 64
LAST_CUTS = [112, 352]
W2_PIECES = [[(0, 256), (256, 512)], [(0, 256), (256, 384), (384, 512)]]


def tile_picked_lora_none_e_kernel(
    tc, xT, w1_words, w1_scales, w2, w3_words, w3_scales, offs, out
):
    nc = tc.nc
    with ExitStack() as ctx:
        sb = ctx.enter_context(tc.tile_pool(name="sb", bufs=1))
        psum = ctx.enter_context(tc.psum_pool(name="psum", bufs=1))

        offsets = sb.tile([P, S // 16], U16, name="offsets")
        w1_codes = sb.tile([P, PASSES, 2 * N], U8, name="w1_codes", align_bytes=256)
        w3_codes = sb.tile([P, 2 * N], U8, name="w3_codes", align_bytes=256)
        w1_sc = sb.tile([P, PASSES, N], U8, name="w1_sc", align_bytes=64)
        w3_sc = sb.tile([P, N], U8, name="w3_sc", align_bytes=64)
        nc.vector.memset(w1_sc[:].bitcast(I32), 0)
        nc.scalar.copy(out=w3_sc[:].bitcast(U32), in_=w1_sc[:, 0, :].bitcast(U32))

        x_rows = xT.rearrange("(z p j) t -> z p (j t)", z=PASSES, p=P, j=PACK)
        w2_rows = w2.rearrange("(z p j) i -> z p j i", z=PASSES, p=P, j=PACK)
        windows, w2_raw = {}, {}

        def load_x(z, j0, j1):
            raw = sb.tile([P, (j1 - j0) * T], F32, name="x_raw_%d_%d" % (z, j0), align_bytes=256)
            nc.sync.dma_start(out=raw[:], in_=x_rows[z][:, j0 * T : j1 * T])
            for j in range(j0, j1):
                windows[z, j] = raw[:, (j - j0) * T : (j - j0 + 1) * T]

        def load_w2(z):
            for lo, hi in W2_PIECES[z]:
                name = "w2_raw_%d_%d" % (z, lo)
                w2_raw[z, lo] = sb.tile([P, PACK, hi - lo], F32, name=name, tag=name, align_bytes=256)
                nc.sync.dma_start(out=w2_raw[z, lo][:], in_=w2_rows[z][:, :, lo:hi])

        for z in range(PASSES):
            for j0, j1 in X_LOADS[z]:
                load_x(z, j0, j1)
                if (z, j0) == (0, 0):
                    nc.sync.dma_start(offsets[:], offs)
        load_w2(0)
        load_w2(1)
        nc.sync.dma_start(out=w1_codes[:].bitcast(I32), in_=w1_words.rearrange("z p c -> p z c").bitcast(I32))
        for q in range(4):
            nc.sync.dma_start(
                out=w1_sc[32 * q : 32 * q + 4, :, :].bitcast(I32),
                in_=w1_scales[:, 4 * q : 4 * q + 4, :].rearrange("z r c -> r z c").bitcast(I32),
            )
        nc.sync.dma_start(out=w3_codes[:].bitcast(I32), in_=w3_words[0].bitcast(I32))
        for q in range(4):
            nc.sync.dma_start(
                out=w3_sc[32 * q : 32 * q + 4, :].bitcast(I32), in_=w3_scales[0, 4 * q : 4 * q + 4, :].bitcast(I32)
            )

        def quantize(codes, sc, values):
            nc.vector.quantize_mx(out=codes.bitcast(FP8X4), scales=sc, in_=values)

        x_bf, x_codes, x_sc, x_tiles = {}, {}, {}, {}

        def group_cols(g):
            return slice(g * GROUP, (g + 1) * GROUP)

        planes = [
            sb.tile([P, PACK, S], F32, name="planes_%d" % z, tag="planes_%d" % z, align_bytes=256) for z in range(PASSES)
        ]

        def gather(z, j, cuts, first=()):
            window = windows[z, j]
            edges = [0, *first, cuts[0]]
            for lo, hi in zip(edges, edges[1:]):
                nc.vector.tensor_copy(out=planes[z][:, j, lo:hi], in_=window.indirect(offsets[:, lo // 16 : hi // 16]))
            for lo, hi in zip(cuts, cuts[1:] + [S]):
                nc.scalar.activation(
                    out=planes[z][:, j, lo:hi], in_=window.indirect(offsets[:, lo // 16 : hi // 16]), func=COPY
                )

        def interleave(z, g, tag, cut):
            x_bf[z, g] = sb.tile([P, GROUP, PACK], BF16, name="x_bf_%d_%d" % (z, g), tag=tag, align_bytes=256)
            dst = x_bf[z, g][:].rearrange("p (c i) j -> p c j i", i=4)
            src = planes[z][:, :, group_cols(g)].rearrange("p j (c i) -> p c j i", i=4)
            if cut > 0:
                nc.scalar.copy(out=dst[:, : cut // 4], in_=src[:, : cut // 4])
            if cut < GROUP:
                nc.vector.tensor_copy(out=dst[:, cut // 4 :], in_=src[:, cut // 4 :])

        def quantize_x(z, groups, tag, order=None):
            width = len(groups) * GROUP
            codes = sb.tile([P, width], U32, name="x_codes_%d_%d" % (z, groups[0]), tag=tag, align_bytes=256)
            sc = sb.tile([P, width], U8, name="x_sc_%d_%d" % (z, groups[0]), align_bytes=64)
            x_tiles[z, groups[0]] = codes, sc
            for e, g in enumerate(groups):
                x_codes[z, g], x_sc[z, g] = codes[:, group_cols(e)], sc[:, group_cols(e)]
            for g in order or groups:
                quantize(x_codes[z, g], x_sc[z, g], x_bf[z, g][:].rearrange("p s j -> p (s j)"))

        w2_codes, w2_sc = {}, {}
        h_acc = [psum.tile([P, PACK, GROUP], F32, name="h_acc_%d" % g) for g in range(GROUPS)]

        def h_pass(z, g, t, start=False, stop=False):
            nc.tensor.matmul_mx(
                out=h_acc[g][:, t, :],
                lhsT=w2_codes[z, t].bitcast(FP8X4),
                lhsT_scale=w2_sc[z, t],
                rhs=x_codes[z, g].bitcast(FP8X4),
                rhs_scale=x_sc[z, g],
                start=start,
                stop=stop,
            )

        def stationary_tiles(z, t0, t1, tag):
            width = (t1 - t0) * P + 2 * CODE_SHIFT
            codes = sb.tile([P, width], U32, name="w2_codes_%d_%d" % (z, t0), tag=tag, align_bytes=256)
            sc = sb.tile([P, t1 - t0, P], U8, name="w2_sc_%d_%d" % (z, t0), align_bytes=64)
            for t in range(t0, t1):
                start = CODE_SHIFT + (t - t0) * P
                w2_codes[z, t], w2_sc[z, t] = codes[:, start : start + P], sc[:, t - t0, :]

        def deal(z, lo, hi, t0, t1, cut):
            name = "w2_dealt_%d_%d_%d" % (z, lo, t0)
            dealt = sb.tile([P, t1 - t0, (hi - lo) // PACK, PACK], BF16, name=name, tag=name, align_bytes=256)
            dst = dealt[:].rearrange("p t m j -> p m j t")
            raw = w2_raw[z, lo][:].rearrange("p j (m t) -> p m j t", t=PACK)[:, :, :, t0:t1]
            m = (cut - lo) // PACK
            if cut < hi:
                nc.vector.tensor_copy(out=dst[:, m:], in_=raw[:, m:])
            if cut > lo:
                nc.scalar.copy(out=dst[:, :m], in_=raw[:, :m])
            return {t: dealt[:, t - t0] for t in range(t0, t1)}

        def quantize_w2(z, lo, hi, dealt, tiles):
            cols = slice(lo // PACK, hi // PACK)
            for t in tiles:
                quantize(w2_codes[z, t][:, cols], w2_sc[z, t][:, cols], dealt[t].rearrange("p m j -> p (m j)"))

        for j in range(PACK):
            gather(0, j, [GATHER_CUTS[0][j]], first=(GROUP,) if j == PACK - 1 else ())
        for g in (3, 0, 2, 1):
            interleave(0, g, "x_bf_0_%d" % g, GROUP if g < 2 else 0)
        quantize_x(0, [0, 1, 2, 3], "x_codes_0", order=(3, 0, 2, 1))
        for j in range(PACK - 1):
            gather(1, j, [GATHER_CUTS[1][j]])
        gather(1, PACK - 1, [GROUP, 2 * GROUP])
        for g in (1, 0, 2, 3):
            interleave(1, g, "x_bf_1_%d" % g, 0)
        first = deal(0, 0, 256, 0, 4, 256)
        second_lo = deal(0, 256, 512, 0, 2, 256 + PAIR_CUT)
        second_hi = deal(0, 256, 512, 2, 4, 512 - PAIR_CUT)
        stationary_tiles(0, 0, 2, "w2_codes_0")
        quantize_w2(0, 0, 256, first, (0, 1))
        quantize_w2(0, 256, 512, second_lo, (0, 1))
        stationary_tiles(0, 2, 4, "w2_dealt_0_256_0")
        quantize_w2(0, 0, 256, first, (2, 3))
        quantize_w2(0, 256, 512, second_hi, (2, 3))
        quantize_x(1, [0, 1], "x_codes_1")
        warm = psum.tile([P, S], F32, name="warm", tag="out_acc_3")
        nc.tensor.matmul_mx(
            out=warm[:],
            lhsT=x_codes[1, 0].bitcast(FP8X4),
            lhsT_scale=x_sc[1, 0],
            rhs=x_tiles[0, 0][0][:].bitcast(FP8X4),
            rhs_scale=x_tiles[0, 0][1][:],
            start=True,
            stop=True,
        )
        put_off = [(GROUPS - 1, t) for t in range(PACK - PUT_OFF, PACK)]
        for t in range(PACK):
            for g in range(GROUPS):
                if (g, t) not in put_off:
                    h_pass(0, g, t, start=(t == 0))
        stationary_tiles(1, 0, 4, "w2_codes_1")
        pieces = [deal(1, 0, 256, 0, 4, LAST_CUTS[0]), deal(1, 256, 384, 0, 4, LAST_CUTS[1])]
        pieces.append({**deal(1, 384, 512, 0, 2, 384), **deal(1, 384, 512, 2, 4, 512)})
        for (lo, hi), dealt in zip(W2_PIECES[1], pieces):
            quantize_w2(1, lo, hi, dealt, range(PACK))
        quantize_x(1, [2, 3], "w2_dealt_1_384_0")
        for g in range(GROUPS):
            h_pass(1, g, 0)
            for t in range(PACK):
                if (g, t) in put_off:
                    h_pass(0, g, t)
            for t in range(1, PACK):
                h_pass(1, g, t, stop=(t == PACK - 1))

        out_acc = [psum.tile([P, GROUP], F32, name="out_acc_%d" % g, tag="out_acc_%d" % g) for g in range(GROUPS)]
        for g in range(GROUPS):
            for z in range(PASSES):
                nc.tensor.matmul_mx(
                    out=out_acc[g][:],
                    lhsT=w1_codes[:, z, :].bitcast(FP4X4),
                    lhsT_scale=w1_sc[:, z, :],
                    rhs=x_codes[z, g].bitcast(FP8X4),
                    rhs_scale=x_sc[z, g],
                    start=(z == 0),
                    stop=False,
                )

        h_bf = [sb.tile([P, GROUP, PACK], BF16, name="h_bf_%d" % g, align_bytes=64) for g in range(GROUPS)]
        for g in range(GROUPS):
            copy = nc.vector.tensor_copy if g % 2 == 0 else nc.scalar.copy
            copy(out=h_bf[g][:], in_=h_acc[g][:].rearrange("p t n -> p n t"))

        for g in range(GROUPS):
            codes = sb.tile([P, GROUP], U32, name="h_codes_%d" % g, align_bytes=64)
            sc = sb.tile([P, GROUP], U8, name="h_sc_%d" % g, align_bytes=64)
            quantize(codes[:], sc[:], h_bf[g][:].rearrange("p n t -> p (n t)"))
            nc.tensor.matmul_mx(
                out=out_acc[g][:],
                lhsT=w3_codes[:].bitcast(FP4X4),
                lhsT_scale=w3_sc[:],
                rhs=codes[:].bitcast(FP8X4),
                rhs_scale=sc[:],
                start=False,
                stop=True,
            )
            first, last = STORE_OF[g]
            if g == first:
                res = sb.tile([P, (last - first + 1) * GROUP], F32, name="res_%d" % g, align_bytes=256)
            copy = nc.vector.tensor_copy if g == GROUPS - 2 else nc.scalar.copy
            copy(out=res[:, group_cols(g - first)], in_=out_acc[g][:])
            if g == last:
                nc.sync.dma_start(out=out[:, first * GROUP : (last + 1) * GROUP], in_=res[:])
